import numpy as np
import ml_dtypes


def mxq(x, axis, fmt="e4m3"):
    dtype, down = {"e4m3": (ml_dtypes.float8_e4m3fn, 7), "e5m2": (ml_dtypes.float8_e5m2, 14)}[fmt]
    v = np.moveaxis(np.asarray(x, np.float32).astype(ml_dtypes.bfloat16).astype(np.float64), axis, -1)
    blocks = v.reshape(v.shape[:-1] + (-1, 32))
    amax = np.abs(blocks).max(-1, keepdims=True)
    byte = np.maximum(np.where(amax > 0, np.frexp(amax)[1] - 1 + 127, 0) - down, 1)
    scale = np.exp2(byte - 127.0)
    codes = (blocks / scale).astype(np.float32).astype(dtype).astype(np.float64)
    return np.moveaxis((codes * scale).reshape(v.shape), -1, axis)


WIDE = False


def mx_kscale(k):
    if not WIDE:
        return np.ones(k)
    levels = np.array([10, -10, 5, -5, 0])
    if k % 512:
        return np.exp2(np.random.permutation(np.resize(levels, k // 32))).repeat(32)
    a = np.empty((k // 512, 16))
    for p in range(k // 512):
        a[p, :8] = np.random.permutation(np.resize(levels, 8))
        for g in range(8):
            far = levels[np.abs(levels - a[p, g]) >= 10]
            a[p, g + 8] = far[np.random.randint(len(far))]
    return np.exp2(a.ravel()).repeat(32)


def f64(x):
    return np.asarray(x).astype(np.float64)


def striped(idx):
    return np.tile(idx.reshape(-1, 16).T, (8, 1)).astype(np.uint16)


def unstriped(offs):
    return offs[:16].T.reshape(-1).astype(np.int64)


E2M1 = np.array([0.0, 0.5, 1.0, 1.5, 2.0, 3.0, 4.0, 6.0, -0.0, -0.5, -1.0, -1.5, -2.0, -3.0, -4.0, -6.0])


def pack_weight(w, fmt):
    k, n = w.shape
    w = f64(np.asarray(w, np.float32).astype(ml_dtypes.bfloat16)).reshape(k // 32, 32, n)
    amax = np.abs(w).max(1)
    if fmt == "e4m3":
        byte = np.frexp(amax)[1] - 1 + 127 - 7
    else:
        mant, ex = np.frexp(amax / 6.0)
        byte = np.where(mant > 0.5, ex, ex - 1) + 127
    byte = np.clip(np.where(amax > 0, byte, 1), 1, 254)
    scaled = (w * np.exp2(127.0 - byte)[:, None, :]).reshape(k, n).astype(np.float32)
    by_word = np.ascontiguousarray(scaled.reshape(k // 512, 128, 4, n).transpose(0, 1, 3, 2))
    if fmt == "e4m3":
        words = by_word.astype(ml_dtypes.float8_e4m3fn).view(np.uint8)
    else:
        c = by_word.astype(ml_dtypes.float4_e2m1fn).view(np.uint8) & 0xF
        words = (c[..., 0::2] | (c[..., 1::2] << 4)).reshape(k // 512, 128, 2 * n)
    return np.ascontiguousarray(words), np.ascontiguousarray(byte.astype(np.uint8).reshape(k // 512, 16, n))


def unpack_weight(words, scales, fmt):
    g, _, n = scales.shape
    words = np.ascontiguousarray(words).reshape(g, 128, n, -1)
    if fmt == "e4m3":
        vals = words.view(ml_dtypes.float8_e4m3fn).astype(np.float64)
    else:
        nib = np.empty((g, 128, n, 4), np.uint8)
        nib[..., 0::2] = words & 0xF
        nib[..., 1::2] = words >> 4
        vals = E2M1[nib]
    vals = vals * np.repeat(np.exp2(scales.astype(np.float64) - 127.0), 8, axis=1)[..., None]
    return vals.transpose(0, 1, 3, 2).reshape(g * 512, n)


def silu(v):
    return v / (1.0 + np.exp(-np.maximum(v, -700.0)))


K, T, E, C, H, N = 512, 512, 12, 128, 512, 384
TOP = 3


def by_expert(wq, xq):
    return np.concatenate([wq[e].T @ xq[:, e * C:(e + 1) * C] for e in range(E)], axis=1)


def setup_inputs():
    n = np.random.standard_normal
    s = mx_kscale(K)[:, None]
    u = mx_kscale(H)
    deal = np.repeat(np.arange(E), C).reshape(TOP, T)[:, np.random.permutation(T)]
    deal = np.take_along_axis(deal, np.argsort(np.random.rand(TOP, T), axis=0), axis=0)
    for _ in range(8):
        s_, t_ = np.random.permutation(T).reshape(2, -1); r = np.random.randint(TOP, size=T // 2); x, y = deal[r, s_].copy(), deal[r, t_].copy()
        ok = ~((deal[:, s_] == y).any(0) | (deal[:, t_] == x).any(0)); deal[r[ok], s_[ok]] = y[ok]; deal[r[ok], t_[ok]] = x[ok]
    order = np.lexsort((np.random.rand(TOP * T), deal.reshape(-1)))
    slot_token = order % T; pos = np.empty(TOP * T, np.int64); pos[order] = np.arange(TOP * T); pos = pos.reshape(TOP, T)
    g = np.random.uniform(0.5, 1.5, (TOP, T)); g = g / g.sum(0)
    x = pack_weight(n((K, T)) * s, "e4m3")
    return {
        "x_words": x[0],
        "x_scales": x[1],
        "w1": (n((E, K, H)) / np.sqrt(K) / s[None] * u[None, None, :]).astype(np.float32),
        "w2": (n((E, H, N)) / np.sqrt(H) / u[None, :, None]).astype(np.float32),
        "gate": np.stack([np.tile(r, (N, 1)) for r in g]).astype(np.float32),
        "offs": striped(slot_token),
        "pos1": striped(pos[0]),
        "pos2": striped(pos[1]),
        "pos3": striped(pos[2]),
    }


def reference(x_words, x_scales, w1, w2, gate, offs, pos1, pos2, pos3):
    idx = unstriped(offs)
    xq = unpack_weight(x_words, x_scales, "e4m3")[:, idx]
    h = silu(by_expert(mxq(f64(w1), 1, "e4m3"), xq))
    y = by_expert(mxq(f64(w2), 1, "e4m3"), mxq(h, 0, "e4m3"))
    return sum(f64(gate[r]) * y[:, unstriped(p)] for r, p in enumerate((pos1, pos2, pos3)))

@@ -1,0 +1,201 @@
+from contextlib import ExitStack
+
+import concourse.mybir as mybir
+
+K, T, E, C, H, N = 512, 512, 12, 128, 512, 384
+TOP = 3
+SLOTS = E * C
+FLOPS = 2 * SLOTS * H * (K + N)
+
+F32 = mybir.dt.float32
+BF16 = mybir.dt.bfloat16
+I32 = mybir.dt.int32
+U32 = mybir.dt.uint32
+U16 = mybir.dt.uint16
+U8 = mybir.dt.uint8
+FP8X4 = mybir.dt.float8_e4m3fn_x4
+MULT = mybir.AluOpType.mult
+ADD = mybir.AluOpType.add
+SILU = mybir.ActivationFunctionType.Silu
+
+P = 128
+PACK = 4
+ROW_TILES = N // P
+WHOLE = 6
+SCALAR_SHARE_WHOLE = 16
+SCALAR_SHARE_SPLIT = 64
+GATHER_EXPERTS = 2
+BANK_GROUPS = [(0, 1, 2), (3, 4, 5), (6, 7, 8), (9, 10), (11,)]
+
+
+def tile_moe_pkd_mlp_silu_kernel(tc, x_words, x_scales, w1, w2, gate, offs, pos1, pos2, pos3, out):
+    nc = tc.nc
+    split = list(range(WHOLE, E))
+    with ExitStack() as ctx:
+        keep = ctx.enter_context(tc.tile_pool(name="keep", bufs=1))
+        raw = ctx.enter_context(tc.tile_pool(name="raw", bufs=1))
+        stage = ctx.enter_context(tc.tile_pool(name="stage", bufs=3))
+        psum = ctx.enter_context(tc.psum_pool(name="psum", bufs=2))
+
+        offs_sb = keep.tile([P, SLOTS // 16], U16, name="offs_sb")
+        pos_sb = [keep.tile([P, T // 16], U16, name="pos_sb%d" % r) for r in range(TOP)]
+        tok_words = keep.tile([P, T], I32, name="tok_words", align_bytes=64)
+        tok_scales = keep.tile([P, T], U8, name="tok_scales", align_bytes=64)
+        slot_words = keep.tile([P, SLOTS], U32, name="slot_words", align_bytes=64)
+        slot_scales = keep.tile([P, SLOTS], U8, name="slot_scales", align_bytes=64)
+        h_words = keep.tile([P, SLOTS], U32, name="h_words", align_bytes=64)
+        h_scales = keep.tile([P, SLOTS], U8, name="h_scales", align_bytes=64)
+        y = [keep.tile([P, SLOTS], F32, name="y%d" % r, align_bytes=64) for r in range(ROW_TILES)]
+
+        w1_raw, w2_raw, gate_sb, banks = {}, {}, {}, {}
+
+        def load_tokens():
+            nc.gpsimd.memset(tok_scales[:], 0)
+            nc.sync.dma_start(offs_sb[:], offs)
+            nc.sync.dma_start(tok_words[:], x_words[0].rearrange("p t r -> p (t r)").bitcast(I32))
+            for q in range(4):
+                nc.sync.dma_start(tok_scales[32 * q : 32 * q + 4, :].bitcast(I32), x_scales[0, 4 * q : 4 * q + 4, :].bitcast(I32))
+
+        def load_w1(e):
+            w1_raw[e] = raw.tile([P, PACK, H], F32, name="w1_raw", tag="big", bufs=E)
+            nc.sync.dma_start(w1_raw[e][:], w1[e].rearrange("(p j) c -> p j c", j=PACK))
+
+        def load_w2_whole(e):
+            tile = raw.tile([P, PACK, N], F32, name="w2_whole", bufs=WHOLE)
+            nc.sync.dma_start(tile[:], w2[e].rearrange("(p j) n -> p j n", j=PACK))
+            w2_raw[e, 0] = tile[:]
+
+        def load_w2_part(e, rt, dest):
+            nc.sync.dma_start(dest, w2[e].rearrange("(p j) n -> p j n", j=PACK)[:, :, rt * P : (rt + 1) * P])
+            w2_raw[e, rt] = dest
+
+        def load_w2_first_part(e):
+            tile = raw.tile([P, PACK, P], F32, name="w2_first", bufs=E - WHOLE)
+            load_w2_part(e, 0, tile[:])
+
+        def load_w2_late_parts(rt):
+            for i0 in range(0, len(split), 3):
+                tile = raw.tile([P, 3, PACK, P], F32, name="w2_late", tag="big", bufs=E)
+                for i, e in enumerate(split[i0 : i0 + 3]):
+                    load_w2_part(e, rt, tile[:, i])
+
+        def load_gate(rt):
+            tile = raw.tile([P, TOP, T], F32, name="gate_sb", tag="big", bufs=E)
+            for r in range(TOP):
+                nc.sync.dma_start(tile[:, r, :], gate[r, rt * P : (rt + 1) * P, :])
+            gate_sb[rt] = tile
+
+        def gather_tokens(e0):
+            cols = slice(e0 * C, (e0 + GATHER_EXPERTS) * C)
+            entries = offs_sb[:, e0 * C // 16 : (e0 + GATHER_EXPERTS) * C // 16]
+            nc.vector.tensor_copy(slot_words[:, cols], tok_words[:].bitcast(U32).indirect(entries))
+            nc.vector.tensor_copy(slot_scales[:, cols], tok_scales[:].indirect(entries))
+
+        def first_layer(e):
+            share = SCALAR_SHARE_WHOLE if e < WHOLE else SCALAR_SHARE_SPLIT
+            grouped = stage.tile([P, PACK * H], BF16, name="w1_bf16", align_bytes=64)
+            dst = grouped[:].rearrange("p (t m j) -> p m t j", t=PACK, j=PACK)
+            src = w1_raw[e][:].rearrange("p j (m t) -> p m t j", t=PACK)
+            nc.vector.tensor_copy(dst[:, share:], src[:, share:])
+            nc.scalar.copy(dst[:, :share], src[:, :share])
+            words = stage.tile([P, H], U32, name="w1_words", align_bytes=64)
+            scales = stage.tile([P, H], U8, name="w1_scales", align_bytes=64)
+            nc.vector.quantize_mx(words[:].bitcast(FP8X4), scales[:], grouped[:])
+            cols = slice(e * C, (e + 1) * C)
+            a = psum.tile([P, PACK, C], F32, name="a_bank")
+            for t in range(PACK):
+                ch = slice(t * P, (t + 1) * P)
+                nc.tensor.matmul_mx(
+                    a[:, t, :],
+                    lhsT=words[:, ch].bitcast(FP8X4),
+                    lhsT_scale=scales[:, ch],
+                    rhs=slot_words[:, cols].bitcast(FP8X4),
+                    rhs_scale=slot_scales[:, cols],
+                    start=True,
+                    stop=True,
+                )
+            h = stage.tile([P, C, PACK], BF16, name="h_bf16", align_bytes=64)
+            nc.scalar.activation(h[:], a[:].rearrange("p t c -> p c t"), SILU)
+            nc.vector.quantize_mx(h_words[:, cols].bitcast(FP8X4), h_scales[:, cols], h[:].rearrange("p c t -> p (c t)"))
+
+        def second_layer(e, rt0):
+            src = w2_raw[e, rt0]
+            width = src.shape[2]
+            grouped = stage.tile([P, width, PACK], BF16, name="w2_bf16", align_bytes=64)
+            nc.scalar.copy(
+                grouped[:].rearrange("p (c i) j -> p c j i", i=4),
+                src.rearrange("p j (c i) -> p c j i", i=4),
+            )
+            words = stage.tile([P, width], U32, name="w2_words", align_bytes=64)
+            scales = stage.tile([P, width], U8, name="w2_scales", align_bytes=64)
+            for c0 in range(0, width, 2 * P):
+                ch = slice(c0, min(c0 + 2 * P, width))
+                nc.vector.quantize_mx(words[:, ch].bitcast(FP8X4), scales[:, ch], grouped[:, ch, :].rearrange("p c j -> p (c j)"))
+            cols = slice(e * C, (e + 1) * C)
+            group = [g for g in BANK_GROUPS if e in g][0]
+            for i in range(width // P):
+                rt = rt0 + i
+                if e == group[0]:
+                    banks[rt] = psum.tile([P, len(group) * C], F32, name="y_bank%d" % rt)
+                place = e - group[0]
+                ch = slice(i * P, (i + 1) * P)
+                nc.tensor.matmul_mx(
+                    banks[rt][:, place * C : (place + 1) * C],
+                    lhsT=words[:, ch].bitcast(FP8X4),
+                    lhsT_scale=scales[:, ch],
+                    rhs=h_words[:, cols].bitcast(FP8X4),
+                    rhs_scale=h_scales[:, cols],
+                    start=True,
+                    stop=True,
+                )
+                if e == group[-1]:
+                    nc.scalar.copy(y[rt][:, group[0] * C : (e + 1) * C], banks[rt][:])
+
+        def combine(rt, pieces):
+            width = T // pieces
+            for s in range(pieces):
+                toks = slice(s * width, (s + 1) * width)
+                terms = []
+                for r in range(TOP):
+                    term = stage.tile([P, width], F32, name="term%d" % r, bufs=2)
+                    entries = pos_sb[r][:, s * width // 16 : (s + 1) * width // 16]
+                    nc.vector.tensor_tensor(term[:], y[rt][:].indirect(entries), gate_sb[rt][:, r, toks], MULT)
+                    terms.append(term)
+                nc.vector.tensor_tensor(terms[0][:], terms[0][:], terms[1][:], ADD)
+                nc.vector.tensor_tensor(terms[0][:], terms[0][:], terms[2][:], ADD)
+                nc.sync.dma_start(out[rt * P : (rt + 1) * P, toks], terms[0][:])
+
+        load_tokens()
+        load_w1(0)
+        for e in range(1, E):
+            load_w1(e)
+            if e - 1 < WHOLE:
+                load_w2_whole(e - 1)
+            elif e - 3 >= WHOLE:
+                load_w2_first_part(e - 3)
+            if e == WHOLE:
+                for r, pos in enumerate((pos1, pos2, pos3)):
+                    nc.sync.dma_start(pos_sb[r][:], pos)
+        for e in range(E - 3, E):
+            load_w2_first_part(e)
+
+        for e in range(E):
+            if e % GATHER_EXPERTS == 0:
+                gather_tokens(e)
+            first_layer(e)
+            if 0 <= e - 1 < WHOLE:
+                second_layer(e - 1, 0)
+            elif e - 3 >= WHOLE:
+                second_layer(e - 3, 0)
+        for e in range(E - 3, E):
+            second_layer(e, 0)
+
+        for rt in range(ROW_TILES):
+            if rt > 0:
+                load_w2_late_parts(rt)
+            load_gate(rt)
+        for rt in range(ROW_TILES):
+            if rt + 1 < ROW_TILES:
+                for e in split:
+                    second_layer(e, rt + 1)
+            combine(rt, 1)

@@ -21,11 +21,12 @@ SILU = mybir.ActivationFunctionType.Silu
 P = 128
 PACK = 4
 ROW_TILES = N // P
-WHOLE = 6
-SCALAR_SHARE_WHOLE = 16
-SCALAR_SHARE_SPLIT = 64
+WHOLE = 4
+LAG = 2
+SCALAR_SHARE = [64, 64, 64, 0, 0, 0, 40, 40, 40, 40, 40, 40]
 GATHER_EXPERTS = 2
-BANK_GROUPS = [(0, 1, 2), (3, 4, 5), (6, 7, 8), (9, 10), (11,)]
+EARLY_GROUPS = [(0, 1, 2, 3), (4, 5, 6, 7), (8, 9, 10), (11,)]
+LATE_GROUPS = [(4, 5, 6, 7), (8, 9), (10,), (11,)]
 
 
 def tile_moe_pkd_mlp_silu_kernel(tc, x_words, x_scales, w1, w2, gate, offs, pos1, pos2, pos3, out):
@@ -40,28 +41,25 @@ def tile_moe_pkd_mlp_silu_kernel(tc, x_words, x_scales, w1, w2, gate, offs, pos1
         offs_sb = keep.tile([P, SLOTS // 16], U16, name="offs_sb")
         pos_sb = [keep.tile([P, T // 16], U16, name="pos_sb%d" % r) for r in range(TOP)]
         tok_words = keep.tile([P, T], I32, name="tok_words", align_bytes=64)
-        tok_scales = keep.tile([P, T], U8, name="tok_scales", align_bytes=64)
-        slot_words = keep.tile([P, SLOTS], U32, name="slot_words", align_bytes=64)
-        slot_scales = keep.tile([P, SLOTS], U8, name="slot_scales", align_bytes=64)
-        h_words = keep.tile([P, SLOTS], U32, name="h_words", align_bytes=64)
-        h_scales = keep.tile([P, SLOTS], U8, name="h_scales", align_bytes=64)
+        tok_scales = keep.tile([P, T // 4], I32, name="tok_scales", align_bytes=64)
+        first_staging = keep.tile([P, (N + C) * PACK], BF16, name="first_staging", align_bytes=64)
         y = [keep.tile([P, SLOTS], F32, name="y%d" % r, align_bytes=64) for r in range(ROW_TILES)]
 
-        w1_raw, w2_raw, gate_sb, banks = {}, {}, {}, {}
+        w1_raw, w2_raw, gate_sb, banks, slots, h_mx, a_banks, late_staging = {}, {}, {}, {}, {}, {}, {}, {}
 
         def load_tokens():
-            nc.gpsimd.memset(tok_scales[:], 0)
+            nc.vector.memset(tok_scales[:], 0)
             nc.sync.dma_start(offs_sb[:], offs)
             nc.sync.dma_start(tok_words[:], x_words[0].rearrange("p t r -> p (t r)").bitcast(I32))
             for q in range(4):
-                nc.sync.dma_start(tok_scales[32 * q : 32 * q + 4, :].bitcast(I32), x_scales[0, 4 * q : 4 * q + 4, :].bitcast(I32))
+                nc.sync.dma_start(tok_scales[32 * q : 32 * q + 4, :], x_scales[0, 4 * q : 4 * q + 4, :].bitcast(I32))
 
         def load_w1(e):
-            w1_raw[e] = raw.tile([P, PACK, H], F32, name="w1_raw", tag="big", bufs=E)
+            w1_raw[e] = raw.tile([P, PACK, H], F32, name="w1_raw", tag="big", bufs=E, align_bytes=64)
             nc.sync.dma_start(w1_raw[e][:], w1[e].rearrange("(p j) c -> p j c", j=PACK))
 
         def load_w2_whole(e):
-            tile = raw.tile([P, PACK, N], F32, name="w2_whole", bufs=WHOLE)
+            tile = raw.tile([P, PACK, N], F32, name="w2_whole", bufs=WHOLE, align_bytes=64)
             nc.sync.dma_start(tile[:], w2[e].rearrange("(p j) n -> p j n", j=PACK))
             w2_raw[e, 0] = tile[:]
 
@@ -70,125 +68,160 @@ def tile_moe_pkd_mlp_silu_kernel(tc, x_words, x_scales, w1, w2, gate, offs, pos1
             w2_raw[e, rt] = dest
 
         def load_w2_first_part(e):
-            tile = raw.tile([P, PACK, P], F32, name="w2_first", bufs=E - WHOLE)
+            tile = raw.tile([P, PACK, P], F32, name="w2_first", bufs=E - WHOLE, align_bytes=64)
             load_w2_part(e, 0, tile[:])
 
         def load_w2_late_parts(rt):
-            for i0 in range(0, len(split), 3):
-                tile = raw.tile([P, 3, PACK, P], F32, name="w2_late", tag="big", bufs=E)
-                for i, e in enumerate(split[i0 : i0 + 3]):
+            for i0 in range(0, len(split), 4):
+                tile = raw.tile([P, 4, PACK, P], F32, name="w2_late", tag="big", bufs=E, align_bytes=64)
+                for i, e in enumerate(split[i0 : i0 + 4]):
                     load_w2_part(e, rt, tile[:, i])
 
         def load_gate(rt):
-            tile = raw.tile([P, TOP, T], F32, name="gate_sb", tag="big", bufs=E)
+            tile = raw.tile([P, TOP, T], F32, name="gate_sb", tag="big", bufs=E, align_bytes=64)
             for r in range(TOP):
                 nc.sync.dma_start(tile[:, r, :], gate[r, rt * P : (rt + 1) * P, :])
             gate_sb[rt] = tile
 
         def gather_tokens(e0):
-            cols = slice(e0 * C, (e0 + GATHER_EXPERTS) * C)
+            words = stage.tile([P, GATHER_EXPERTS * C], U32, name="slot_words", align_bytes=64, bufs=2)
+            scales = stage.tile([P, GATHER_EXPERTS * C], U8, name="slot_scales", align_bytes=64, bufs=2)
             entries = offs_sb[:, e0 * C // 16 : (e0 + GATHER_EXPERTS) * C // 16]
-            nc.vector.tensor_copy(slot_words[:, cols], tok_words[:].bitcast(U32).indirect(entries))
-            nc.vector.tensor_copy(slot_scales[:, cols], tok_scales[:].indirect(entries))
+            nc.vector.tensor_copy(words[:], tok_words[:].bitcast(U32).indirect(entries))
+            nc.vector.tensor_copy(scales[:], tok_scales[:].bitcast(U8).indirect(entries))
+            for i in range(GATHER_EXPERTS):
+                slots[e0 + i] = (words[:, i * C : (i + 1) * C], scales[:, i * C : (i + 1) * C])
 
         def first_layer(e):
-            share = SCALAR_SHARE_WHOLE if e < WHOLE else SCALAR_SHARE_SPLIT
+            share = SCALAR_SHARE[e]
             grouped = stage.tile([P, PACK * H], BF16, name="w1_bf16", align_bytes=64)
             dst = grouped[:].rearrange("p (t m j) -> p m t j", t=PACK, j=PACK)
             src = w1_raw[e][:].rearrange("p j (m t) -> p m t j", t=PACK)
             nc.vector.tensor_copy(dst[:, share:], src[:, share:])
-            nc.scalar.copy(dst[:, :share], src[:, :share])
+            if share:
+                nc.scalar.copy(dst[:, :share], src[:, :share])
             words = stage.tile([P, H], U32, name="w1_words", align_bytes=64)
             scales = stage.tile([P, H], U8, name="w1_scales", align_bytes=64)
             nc.vector.quantize_mx(words[:].bitcast(FP8X4), scales[:], grouped[:])
-            cols = slice(e * C, (e + 1) * C)
-            a = psum.tile([P, PACK, C], F32, name="a_bank")
+            a = psum.tile([P, PACK, C], F32, name="a_bank", bufs=3)
             for t in range(PACK):
                 ch = slice(t * P, (t + 1) * P)
                 nc.tensor.matmul_mx(
                     a[:, t, :],
                     lhsT=words[:, ch].bitcast(FP8X4),
                     lhsT_scale=scales[:, ch],
-                    rhs=slot_words[:, cols].bitcast(FP8X4),
-                    rhs_scale=slot_scales[:, cols],
+                    rhs=slots[e][0].bitcast(FP8X4),
+                    rhs_scale=slots[e][1],
                     start=True,
                     stop=True,
                 )
-            h = stage.tile([P, C, PACK], BF16, name="h_bf16", align_bytes=64)
-            nc.scalar.activation(h[:], a[:].rearrange("p t c -> p c t"), SILU)
-            nc.vector.quantize_mx(h_words[:, cols].bitcast(FP8X4), h_scales[:, cols], h[:].rearrange("p c t -> p (c t)"))
+            a_banks[e] = a
 
-        def second_layer(e, rt0):
-            src = w2_raw[e, rt0]
-            width = src.shape[2]
-            grouped = stage.tile([P, width, PACK], BF16, name="w2_bf16", align_bytes=64)
-            nc.scalar.copy(
-                grouped[:].rearrange("p (c i) j -> p c j i", i=4),
-                src.rearrange("p j (c i) -> p c j i", i=4),
+        def staging(e):
+            width = (N if e < WHOLE else P) + C
+            if e == 0:
+                flat = first_staging[:]
+            else:
+                flat = w2_raw[e - 1, 0].rearrange("p j n -> p (j n)").bitcast(BF16)
+            return flat[:, : width * PACK].rearrange("p (c j) -> p c j", j=PACK)
+
+        def activate(e):
+            dst = staging(e)
+            nc.scalar.activation(dst[:, dst.shape[1] - C :, :], a_banks[e][:].rearrange("p t c -> p c t"), SILU)
+
+        def round_w2(dst, src):
+            nc.scalar.copy(dst.rearrange("p (c i) j -> p c j i", i=4), src.rearrange("p j (c i) -> p c j i", i=4))
+
+        def multiply_w2(e, rt, words, scales, groups):
+            group = [g for g in groups if e in g][0]
+            if e == group[0]:
+                banks[rt] = psum.tile([P, len(group) * C], F32, name="y_bank", bufs=5)
+            place = e - group[0]
+            nc.tensor.matmul_mx(
+                banks[rt][:, place * C : (place + 1) * C],
+                lhsT=words.bitcast(FP8X4),
+                lhsT_scale=scales,
+                rhs=h_mx[e][0].bitcast(FP8X4),
+                rhs_scale=h_mx[e][1],
+                start=True,
+                stop=True,
             )
-            words = stage.tile([P, width], U32, name="w2_words", align_bytes=64)
-            scales = stage.tile([P, width], U8, name="w2_scales", align_bytes=64)
-            for c0 in range(0, width, 2 * P):
-                ch = slice(c0, min(c0 + 2 * P, width))
-                nc.vector.quantize_mx(words[:, ch].bitcast(FP8X4), scales[:, ch], grouped[:, ch, :].rearrange("p c j -> p (c j)"))
-            cols = slice(e * C, (e + 1) * C)
-            group = [g for g in BANK_GROUPS if e in g][0]
-            for i in range(width // P):
-                rt = rt0 + i
-                if e == group[0]:
-                    banks[rt] = psum.tile([P, len(group) * C], F32, name="y_bank%d" % rt)
-                place = e - group[0]
-                ch = slice(i * P, (i + 1) * P)
-                nc.tensor.matmul_mx(
-                    banks[rt][:, place * C : (place + 1) * C],
-                    lhsT=words[:, ch].bitcast(FP8X4),
-                    lhsT_scale=scales[:, ch],
-                    rhs=h_words[:, cols].bitcast(FP8X4),
-                    rhs_scale=h_scales[:, cols],
-                    start=True,
-                    stop=True,
-                )
-                if e == group[-1]:
-                    nc.scalar.copy(y[rt][:, group[0] * C : (e + 1) * C], banks[rt][:])
+            if e == group[-1]:
+                nc.scalar.copy(y[rt][:, group[0] * C : (e + 1) * C], banks[rt][:])
 
-        def combine(rt, pieces):
-            width = T // pieces
-            for s in range(pieces):
-                toks = slice(s * width, (s + 1) * width)
-                terms = []
+        def second_layer_early(e):
+            dst = staging(e)
+            width = dst.shape[1] - C
+            round_w2(dst[:, :width, :], w2_raw[e, 0])
+            kind, bufs = ("whole", 2) if e < WHOLE else ("first", E - WHOLE)
+            words = stage.tile([P, width + C], U32, name="words_" + kind, align_bytes=64, bufs=bufs)
+            scales = stage.tile([P, width + C], U8, name="scales_" + kind, align_bytes=64, bufs=bufs)
+            nc.vector.quantize_mx(words[:].bitcast(FP8X4), scales[:], dst.rearrange("p c j -> p (c j)"))
+            h_mx[e] = (words[:, width:], scales[:, width:])
+            for rt in range(width // P):
+                ch = slice(rt * P, (rt + 1) * P)
+                multiply_w2(e, rt, words[:, ch], scales[:, ch], EARLY_GROUPS)
+
+        def second_layer_late(rt):
+            late = raw.tile([P, len(split) * P, PACK], BF16, name="late_bf16", tag="big", bufs=E, align_bytes=64)
+            late_staging[rt] = late
+            for group in LATE_GROUPS:
+                width = len(group) * P
+                c0 = (group[0] - WHOLE) * P
+                for i, e in enumerate(group):
+                    round_w2(late[:, c0 + i * P : c0 + (i + 1) * P, :], w2_raw[e, rt])
+                words = stage.tile([P, width], U32, name="words_late", align_bytes=64, bufs=4)
+                scales = stage.tile([P, width], U8, name="scales_late", align_bytes=64, bufs=4)
+                nc.vector.quantize_mx(words[:].bitcast(FP8X4), scales[:], late[:, c0 : c0 + width, :].rearrange("p c j -> p (c j)"))
+                for i, e in enumerate(group):
+                    ch = slice(i * P, (i + 1) * P)
+                    multiply_w2(e, rt, words[:, ch], scales[:, ch], LATE_GROUPS)
+
+        def weighted_gather(dst, rt, r, toks):
+            entries = pos_sb[r][:, toks.start // 16 : toks.stop // 16]
+            nc.vector.tensor_tensor(dst, y[rt][:].indirect(entries), gate_sb[rt][:, r, toks], MULT)
+
+        def combine(rt):
+            terms = [stage.tile([P, T], F32, name="term%d" % r, bufs=2)[:] for r in range(TOP - 1)]
+            if rt + 1 < ROW_TILES:
+                spent = late_staging[rt + 1][:].rearrange("p c j -> p (c j)").bitcast(F32)
+                terms.append(spent[:, :T])
+                total = spent[:, 3 * T :]
+                pieces = [slice(0, T)]
+            else:
+                terms.append(stage.tile([P, T], F32, name="last_term", bufs=1)[:])
+                total = terms[0]
+                pieces = [slice(0, T // 2), slice(T // 2, T)]
+            for toks in pieces:
                 for r in range(TOP):
-                    term = stage.tile([P, width], F32, name="term%d" % r, bufs=2)
-                    entries = pos_sb[r][:, s * width // 16 : (s + 1) * width // 16]
-                    nc.vector.tensor_tensor(term[:], y[rt][:].indirect(entries), gate_sb[rt][:, r, toks], MULT)
-                    terms.append(term)
-                nc.vector.tensor_tensor(terms[0][:], terms[0][:], terms[1][:], ADD)
-                nc.vector.tensor_tensor(terms[0][:], terms[0][:], terms[2][:], ADD)
-                nc.sync.dma_start(out[rt * P : (rt + 1) * P, toks], terms[0][:])
+                    weighted_gather(terms[r][:, toks], rt, r, toks)
+                nc.vector.tensor_tensor(total[:, toks], terms[0][:, toks], terms[1][:, toks], ADD)
+                nc.vector.tensor_tensor(total[:, toks], total[:, toks], terms[2][:, toks], ADD)
+                nc.sync.dma_start(out[rt * P : (rt + 1) * P, toks], total[:, toks])
 
         load_tokens()
-        load_w1(0)
-        for e in range(1, E):
-            load_w1(e)
-            if e - 1 < WHOLE:
-                load_w2_whole(e - 1)
-            elif e - 3 >= WHOLE:
-                load_w2_first_part(e - 3)
-            if e == WHOLE:
+        for step in range(E + LAG):
+            if step < E:
+                load_w1(step)
+            if step == WHOLE:
                 for r, pos in enumerate((pos1, pos2, pos3)):
                     nc.sync.dma_start(pos_sb[r][:], pos)
-        for e in range(E - 3, E):
-            load_w2_first_part(e)
+            if 0 <= step - LAG < WHOLE:
+                load_w2_whole(step - LAG)
+            elif step - LAG >= WHOLE:
+                load_w2_first_part(step - LAG)
 
-        for e in range(E):
-            if e % GATHER_EXPERTS == 0:
-                gather_tokens(e)
-            first_layer(e)
-            if 0 <= e - 1 < WHOLE:
-                second_layer(e - 1, 0)
-            elif e - 3 >= WHOLE:
-                second_layer(e - 3, 0)
-        for e in range(E - 3, E):
-            second_layer(e, 0)
+        for step in range(E + LAG):
+            if step < E:
+                if step % GATHER_EXPERTS == 0:
+                    gather_tokens(step)
+                first_layer(step)
+            if step == 0:
+                activate(0)
+            if step >= LAG:
+                second_layer_early(step - LAG)
+                if step - LAG + 1 < E:
+                    activate(step - LAG + 1)
 
         for rt in range(ROW_TILES):
             if rt > 0:
@@ -196,6 +229,5 @@ def tile_moe_pkd_mlp_silu_kernel(tc, x_words, x_scales, w1, w2, gate, offs, pos1
             load_gate(rt)
         for rt in range(ROW_TILES):
             if rt + 1 < ROW_TILES:
-                for e in split:
-                    second_layer(e, rt + 1)
-            combine(rt, 1)
+                second_layer_late(rt + 1)
+            combine(rt)

@@ -95,8 +95,8 @@ def tile_moe_pkd_mlp_silu_kernel(tc, x_words, x_scales, w1, w2, gate, offs, pos1
         def first_layer(e):
             share = SCALAR_SHARE[e]
             grouped = stage.tile([P, PACK * H], BF16, name="w1_bf16", align_bytes=64)
-            dst = grouped[:].rearrange("p (t m j) -> p m t j", t=PACK, j=PACK)
-            src = w1_raw[e][:].rearrange("p j (m t) -> p m t j", t=PACK)
+            dst = grouped[:].rearrange("p (t m j) -> p m j t", t=PACK, j=PACK)
+            src = w1_raw[e][:].rearrange("p j (m t) -> p m j t", t=PACK)
             nc.vector.tensor_copy(dst[:, share:], src[:, share:])
             if share:
                 nc.scalar.copy(dst[:, :share], src[:, :share])
@@ -177,27 +177,27 @@ def tile_moe_pkd_mlp_silu_kernel(tc, x_words, x_scales, w1, w2, gate, offs, pos1
                     ch = slice(i * P, (i + 1) * P)
                     multiply_w2(e, rt, words[:, ch], scales[:, ch], LATE_GROUPS)
 
-        def weighted_gather(dst, rt, r, toks):
-            entries = pos_sb[r][:, toks.start // 16 : toks.stop // 16]
-            nc.vector.tensor_tensor(dst, y[rt][:].indirect(entries), gate_sb[rt][:, r, toks], MULT)
-
         def combine(rt):
             terms = [stage.tile([P, T], F32, name="term%d" % r, bufs=2)[:] for r in range(TOP - 1)]
-            if rt + 1 < ROW_TILES:
-                spent = late_staging[rt + 1][:].rearrange("p c j -> p (c j)").bitcast(F32)
-                terms.append(spent[:, :T])
-                total = spent[:, 3 * T :]
-                pieces = [slice(0, T)]
-            else:
+            halves = [slice(0, T // 2), slice(T // 2, T)]
+            last = rt + 1 == ROW_TILES
+            if last:
                 terms.append(stage.tile([P, T], F32, name="last_term", bufs=1)[:])
                 total = terms[0]
-                pieces = [slice(0, T // 2), slice(T // 2, T)]
-            for toks in pieces:
-                for r in range(TOP):
-                    weighted_gather(terms[r][:, toks], rt, r, toks)
+            else:
+                spent = late_staging[rt + 1][:].rearrange("p c j -> p (c j)").bitcast(F32)
+                terms.append(spent[:, :T])
+                total = spent[:, spent.shape[1] - T :]
+            for r in range(TOP):
+                nc.vector.tensor_tensor(terms[r], y[rt][:].indirect(pos_sb[r][:]), gate_sb[rt][:, r, :], MULT)
+            for toks in halves:
                 nc.vector.tensor_tensor(total[:, toks], terms[0][:, toks], terms[1][:, toks], ADD)
+            for toks in halves:
                 nc.vector.tensor_tensor(total[:, toks], total[:, toks], terms[2][:, toks], ADD)
-                nc.sync.dma_start(out[rt * P : (rt + 1) * P, toks], total[:, toks])
+                if last:
+                    nc.sync.dma_start(out[rt * P : (rt + 1) * P, toks], total[:, toks])
+            if not last:
+                nc.sync.dma_start(out[rt * P : (rt + 1) * P, :], total)
 
         load_tokens()
         for step in range(E + LAG):

@@ -22,11 +22,12 @@ P = 128
 PACK = 4
 ROW_TILES = N // P
 WHOLE = 4
-LAG = 2
-SCALAR_SHARE = [64, 64, 64, 0, 0, 0, 40, 40, 40, 40, 40, 40]
+LAG = 4
+VECTOR_ROUNDS = 3
+SCALAR_SHARE = [72, 72, 72, 72, 24, 24, 24, 24, 48, 48, 48, 64]
 GATHER_EXPERTS = 2
 EARLY_GROUPS = [(0, 1, 2, 3), (4, 5, 6, 7), (8, 9, 10), (11,)]
-LATE_GROUPS = [(4, 5, 6, 7), (8, 9), (10,), (11,)]
+LATE_GROUPS = {1: [(4, 5, 6, 7), (8, 9, 10, 11)], 2: [(4, 5, 6, 7), (8, 9), (10,), (11,)]}
 
 
 def tile_moe_pkd_mlp_silu_kernel(tc, x_words, x_scales, w1, w2, gate, offs, pos1, pos2, pos3, out):
@@ -42,7 +43,6 @@ def tile_moe_pkd_mlp_silu_kernel(tc, x_words, x_scales, w1, w2, gate, offs, pos1
         pos_sb = [keep.tile([P, T // 16], U16, name="pos_sb%d" % r) for r in range(TOP)]
         tok_words = keep.tile([P, T], I32, name="tok_words", align_bytes=64)
         tok_scales = keep.tile([P, T // 4], I32, name="tok_scales", align_bytes=64)
-        first_staging = keep.tile([P, (N + C) * PACK], BF16, name="first_staging", align_bytes=64)
         y = [keep.tile([P, SLOTS], F32, name="y%d" % r, align_bytes=64) for r in range(ROW_TILES)]
 
         w1_raw, w2_raw, gate_sb, banks, slots, h_mx, a_banks, late_staging = {}, {}, {}, {}, {}, {}, {}, {}
@@ -119,18 +119,18 @@ def tile_moe_pkd_mlp_silu_kernel(tc, x_words, x_scales, w1, w2, gate, offs, pos1
 
         def staging(e):
             width = (N if e < WHOLE else P) + C
-            if e == 0:
-                flat = first_staging[:]
+            if e < LAG - 1:
+                flat = w1_raw[e + 1][:].rearrange("p j c -> p (j c)").bitcast(BF16)
             else:
-                flat = w2_raw[e - 1, 0].rearrange("p j n -> p (j n)").bitcast(BF16)
+                flat = w2_raw[e - (LAG - 1), 0].rearrange("p j n -> p (j n)").bitcast(BF16)
             return flat[:, : width * PACK].rearrange("p (c j) -> p c j", j=PACK)
 
         def activate(e):
             dst = staging(e)
             nc.scalar.activation(dst[:, dst.shape[1] - C :, :], a_banks[e][:].rearrange("p t c -> p c t"), SILU)
 
-        def round_w2(dst, src):
-            nc.scalar.copy(dst.rearrange("p (c i) j -> p c j i", i=4), src.rearrange("p j (c i) -> p c j i", i=4))
+        def round_w2(dst, src, copy):
+            copy(dst.rearrange("p (c i) j -> p c j i", i=4), src.rearrange("p j (c i) -> p c j i", i=4))
 
         def multiply_w2(e, rt, words, scales, groups):
             group = [g for g in groups if e in g][0]
@@ -152,7 +152,7 @@ def tile_moe_pkd_mlp_silu_kernel(tc, x_words, x_scales, w1, w2, gate, offs, pos1
         def second_layer_early(e):
             dst = staging(e)
             width = dst.shape[1] - C
-            round_w2(dst[:, :width, :], w2_raw[e, 0])
+            round_w2(dst[:, :width, :], w2_raw[e, 0], nc.vector.tensor_copy if e >= E - VECTOR_ROUNDS else nc.scalar.copy)
             kind, bufs = ("whole", 2) if e < WHOLE else ("first", E - WHOLE)
             words = stage.tile([P, width + C], U32, name="words_" + kind, align_bytes=64, bufs=bufs)
             scales = stage.tile([P, width + C], U8, name="scales_" + kind, align_bytes=64, bufs=bufs)
@@ -165,17 +165,17 @@ def tile_moe_pkd_mlp_silu_kernel(tc, x_words, x_scales, w1, w2, gate, offs, pos1
         def second_layer_late(rt):
             late = raw.tile([P, len(split) * P, PACK], BF16, name="late_bf16", tag="big", bufs=E, align_bytes=64)
             late_staging[rt] = late
-            for group in LATE_GROUPS:
+            for group in LATE_GROUPS[rt]:
                 width = len(group) * P
                 c0 = (group[0] - WHOLE) * P
                 for i, e in enumerate(group):
-                    round_w2(late[:, c0 + i * P : c0 + (i + 1) * P, :], w2_raw[e, rt])
+                    round_w2(late[:, c0 + i * P : c0 + (i + 1) * P, :], w2_raw[e, rt], nc.scalar.copy)
                 words = stage.tile([P, width], U32, name="words_late", align_bytes=64, bufs=4)
                 scales = stage.tile([P, width], U8, name="scales_late", align_bytes=64, bufs=4)
                 nc.vector.quantize_mx(words[:].bitcast(FP8X4), scales[:], late[:, c0 : c0 + width, :].rearrange("p c j -> p (c j)"))
                 for i, e in enumerate(group):
                     ch = slice(i * P, (i + 1) * P)
-                    multiply_w2(e, rt, words[:, ch], scales[:, ch], LATE_GROUPS)
+                    multiply_w2(e, rt, words[:, ch], scales[:, ch], LATE_GROUPS[rt])
 
         def combine(rt):
             terms = [stage.tile([P, T], F32, name="term%d" % r, bufs=2)[:] for r in range(TOP - 1)]
@@ -203,7 +203,7 @@ def tile_moe_pkd_mlp_silu_kernel(tc, x_words, x_scales, w1, w2, gate, offs, pos1
         for step in range(E + LAG):
             if step < E:
                 load_w1(step)
-            if step == WHOLE:
+            if step == 4:
                 for r, pos in enumerate((pos1, pos2, pos3)):
                     nc.sync.dma_start(pos_sb[r][:], pos)
             if 0 <= step - LAG < WHOLE:
@@ -216,12 +216,10 @@ def tile_moe_pkd_mlp_silu_kernel(tc, x_words, x_scales, w1, w2, gate, offs, pos1
                 if step % GATHER_EXPERTS == 0:
                     gather_tokens(step)
                 first_layer(step)
-            if step == 0:
-                activate(0)
             if step >= LAG:
                 second_layer_early(step - LAG)
-                if step - LAG + 1 < E:
-                    activate(step - LAG + 1)
+            if 1 <= step <= E:
+                activate(step - 1)
 
         for rt in range(ROW_TILES):
             if rt > 0:

@@ -1,6 +1,7 @@
 from contextlib import ExitStack
 
 import concourse.mybir as mybir
+from concourse.masks import make_identity
 
 K, T, E, C, H, N = 512, 512, 12, 128, 512, 384
 TOP = 3
@@ -21,18 +22,18 @@ SILU = mybir.ActivationFunctionType.Silu
 P = 128
 PACK = 4
 ROW_TILES = N // P
-WHOLE = 4
-LAG = 4
-VECTOR_ROUNDS = 3
-SCALAR_SHARE = [72, 72, 72, 72, 24, 24, 24, 24, 48, 48, 48, 64]
-GATHER_EXPERTS = 2
-EARLY_GROUPS = [(0, 1, 2, 3), (4, 5, 6, 7), (8, 9, 10), (11,)]
-LATE_GROUPS = {1: [(4, 5, 6, 7), (8, 9, 10, 11)], 2: [(4, 5, 6, 7), (8, 9), (10,), (11,)]}
+SCALAR_ALONE = 3
+WHOLE = 6
+BANK = 4
+GATHER_EXPERTS = 3
 
 
 def tile_moe_pkd_mlp_silu_kernel(tc, x_words, x_scales, w1, w2, gate, offs, pos1, pos2, pos3, out):
     nc = tc.nc
-    split = list(range(WHOLE, E))
+    early_groups = [(0, 1, 2, 3), (4, 5, 6, 7), (8, 9, 10), (11,)]
+    whole_groups = [(0, 1, 2, 3), (4, 5)]
+    late_groups = [(6, 7, 8, 9), (10, 11)]
+    whole_after = {max(e + 2, 2 * e): e for e in range(WHOLE)}
     with ExitStack() as ctx:
         keep = ctx.enter_context(tc.tile_pool(name="keep", bufs=1))
         raw = ctx.enter_context(tc.tile_pool(name="raw", bufs=1))
@@ -43,9 +44,15 @@ def tile_moe_pkd_mlp_silu_kernel(tc, x_words, x_scales, w1, w2, gate, offs, pos1
         pos_sb = [keep.tile([P, T // 16], U16, name="pos_sb%d" % r) for r in range(TOP)]
         tok_words = keep.tile([P, T], I32, name="tok_words", align_bytes=64)
         tok_scales = keep.tile([P, T // 4], I32, name="tok_scales", align_bytes=64)
+        slot_words = keep.tile([P, SLOTS], U32, name="slot_words", align_bytes=64)
+        slot_scales = keep.tile([P, SLOTS], U8, name="slot_scales", align_bytes=64)
         y = [keep.tile([P, SLOTS], F32, name="y%d" % r, align_bytes=64) for r in range(ROW_TILES)]
+        identity = keep.tile([P, P], F32, name="identity", align_bytes=64)
+        warm = keep.tile([P, 1], F32, name="warm")
+        gate_cols = keep.tile([P, TOP, T // P], F32, name="gate_cols", align_bytes=64)
+        gate_sb = keep.tile([P, TOP, T], F32, name="gate_sb", align_bytes=64)
 
-        w1_raw, w2_raw, gate_sb, banks, slots, h_mx, a_banks, late_staging = {}, {}, {}, {}, {}, {}, {}, {}
+        w1_raw, w2_raw, banks, h_mx, a_banks, late_staging = {}, {}, {}, {}, {}, {}
 
         def load_tokens():
             nc.vector.memset(tok_scales[:], 0)
@@ -53,6 +60,18 @@ def tile_moe_pkd_mlp_silu_kernel(tc, x_words, x_scales, w1, w2, gate, offs, pos1
             nc.sync.dma_start(tok_words[:], x_words[0].rearrange("p t r -> p (t r)").bitcast(I32))
             for q in range(4):
                 nc.sync.dma_start(tok_scales[32 * q : 32 * q + 4, :], x_scales[0, 4 * q : 4 * q + 4, :].bitcast(I32))
+
+        def load_gate():
+            nc.sync.dma_start(gate_cols[:], gate[:, 0, :].rearrange("r (p c) -> p r c", p=P))
+
+        def spread_gate():
+            make_identity(nc, identity[:])
+            nc.scalar.activation(warm[:], identity[:, 0:1], SILU)
+            for r in range(TOP):
+                bank = psum.tile([P, T], F32, name="y_bank", bufs=5)
+                for c in range(T // P):
+                    nc.tensor.transpose(bank[:, c * P : (c + 1) * P], gate_cols[:, r, c : c + 1].to_broadcast([P, P]), identity[:])
+                nc.scalar.copy(gate_sb[:, r, :].rearrange("n (p c) -> n p c", p=P), bank[:].rearrange("n (c p) -> n p c", p=P))
 
         def load_w1(e):
             w1_raw[e] = raw.tile([P, PACK, H], F32, name="w1_raw", tag="big", bufs=E, align_bytes=64)
@@ -72,46 +91,40 @@ def tile_moe_pkd_mlp_silu_kernel(tc, x_words, x_scales, w1, w2, gate, offs, pos1
             load_w2_part(e, 0, tile[:])
 
         def load_w2_late_parts(rt):
-            for i0 in range(0, len(split), 4):
-                tile = raw.tile([P, 4, PACK, P], F32, name="w2_late", tag="big", bufs=E, align_bytes=64)
-                for i, e in enumerate(split[i0 : i0 + 4]):
-                    load_w2_part(e, rt, tile[:, i])
-
-        def load_gate(rt):
-            tile = raw.tile([P, TOP, T], F32, name="gate_sb", tag="big", bufs=E, align_bytes=64)
-            for r in range(TOP):
-                nc.sync.dma_start(tile[:, r, :], gate[r, rt * P : (rt + 1) * P, :])
-            gate_sb[rt] = tile
+            for group in late_groups:
+                tile = raw.tile([P, len(group), PACK, P], F32, name="w2_late", tag="big", bufs=E, align_bytes=64)
+                for i, e in enumerate(group):
+                    if e == E - 1:
+                        dest = y[rt][:, WHOLE * C : (WHOLE + BANK) * C].rearrange("p (j n) -> p j n", j=PACK)
+                    else:
+                        dest = tile[:, i]
+                    load_w2_part(e, rt, dest)
 
         def gather_tokens(e0):
-            words = stage.tile([P, GATHER_EXPERTS * C], U32, name="slot_words", align_bytes=64, bufs=2)
-            scales = stage.tile([P, GATHER_EXPERTS * C], U8, name="slot_scales", align_bytes=64, bufs=2)
+            cols = slice(e0 * C, (e0 + GATHER_EXPERTS) * C)
             entries = offs_sb[:, e0 * C // 16 : (e0 + GATHER_EXPERTS) * C // 16]
-            nc.vector.tensor_copy(words[:], tok_words[:].bitcast(U32).indirect(entries))
-            nc.vector.tensor_copy(scales[:], tok_scales[:].bitcast(U8).indirect(entries))
-            for i in range(GATHER_EXPERTS):
-                slots[e0 + i] = (words[:, i * C : (i + 1) * C], scales[:, i * C : (i + 1) * C])
+            nc.vector.tensor_copy(slot_words[:, cols], tok_words[:].bitcast(U32).indirect(entries))
+            nc.vector.tensor_copy(slot_scales[:, cols], tok_scales[:].bitcast(U8).indirect(entries))
 
         def first_layer(e):
-            share = SCALAR_SHARE[e]
             grouped = stage.tile([P, PACK * H], BF16, name="w1_bf16", align_bytes=64)
             dst = grouped[:].rearrange("p (t m j) -> p m j t", t=PACK, j=PACK)
             src = w1_raw[e][:].rearrange("p j (m t) -> p m j t", t=PACK)
-            nc.vector.tensor_copy(dst[:, share:], src[:, share:])
-            if share:
-                nc.scalar.copy(dst[:, :share], src[:, :share])
+            copy = nc.scalar.copy if e < SCALAR_ALONE else nc.vector.tensor_copy
+            copy(dst, src)
             words = stage.tile([P, H], U32, name="w1_words", align_bytes=64)
             scales = stage.tile([P, H], U8, name="w1_scales", align_bytes=64)
             nc.vector.quantize_mx(words[:].bitcast(FP8X4), scales[:], grouped[:])
             a = psum.tile([P, PACK, C], F32, name="a_bank", bufs=3)
+            cols = slice(e * C, (e + 1) * C)
             for t in range(PACK):
                 ch = slice(t * P, (t + 1) * P)
                 nc.tensor.matmul_mx(
                     a[:, t, :],
                     lhsT=words[:, ch].bitcast(FP8X4),
                     lhsT_scale=scales[:, ch],
-                    rhs=slots[e][0].bitcast(FP8X4),
-                    rhs_scale=slots[e][1],
+                    rhs=slot_words[:, cols].bitcast(FP8X4),
+                    rhs_scale=slot_scales[:, cols],
                     start=True,
                     stop=True,
                 )
@@ -119,10 +132,14 @@ def tile_moe_pkd_mlp_silu_kernel(tc, x_words, x_scales, w1, w2, gate, offs, pos1
 
         def staging(e):
             width = (N if e < WHOLE else P) + C
-            if e < LAG - 1:
-                flat = w1_raw[e + 1][:].rearrange("p j c -> p (j c)").bitcast(BF16)
+            if e < SCALAR_ALONE - 1:
+                flat = w1_raw[SCALAR_ALONE - 1][:].rearrange("p j c -> p (j c)").bitcast(BF16)[:, e * PACK * H :]
+            elif e in whole_after:
+                flat = w2_raw[whole_after[e], 0].rearrange("p j n -> p (j n)").bitcast(BF16)
+            elif e + 1 in whole_after:
+                flat = w2_raw[whole_after[e + 1], 0].rearrange("p j n -> p (j n)").bitcast(BF16)[:, PACK * (P + C) :]
             else:
-                flat = w2_raw[e - (LAG - 1), 0].rearrange("p j n -> p (j n)").bitcast(BF16)
+                flat = w2_raw[E - 4, 0].rearrange("p j n -> p (j n)").bitcast(BF16)
             return flat[:, : width * PACK].rearrange("p (c j) -> p c j", j=PACK)
 
         def activate(e):
@@ -135,10 +152,10 @@ def tile_moe_pkd_mlp_silu_kernel(tc, x_words, x_scales, w1, w2, gate, offs, pos1
         def multiply_w2(e, rt, words, scales, groups):
             group = [g for g in groups if e in g][0]
             if e == group[0]:
-                banks[rt] = psum.tile([P, len(group) * C], F32, name="y_bank", bufs=5)
+                banks[rt, group] = psum.tile([P, len(group) * C], F32, name="y_bank", bufs=5)
             place = e - group[0]
             nc.tensor.matmul_mx(
-                banks[rt][:, place * C : (place + 1) * C],
+                banks[rt, group][:, place * C : (place + 1) * C],
                 lhsT=words.bitcast(FP8X4),
                 lhsT_scale=scales,
                 rhs=h_mx[e][0].bitcast(FP8X4),
@@ -146,13 +163,17 @@ def tile_moe_pkd_mlp_silu_kernel(tc, x_words, x_scales, w1, w2, gate, offs, pos1
                 start=True,
                 stop=True,
             )
-            if e == group[-1]:
-                nc.scalar.copy(y[rt][:, group[0] * C : (e + 1) * C], banks[rt][:])
+            if e == group[-1] and group != late_groups[0]:
+                empty_bank(rt, group)
+
+        def empty_bank(rt, group):
+            copy = nc.vector.tensor_copy if group == (E - 1,) else nc.scalar.copy
+            copy(y[rt][:, group[0] * C : (group[-1] + 1) * C], banks[rt, group][:])
 
         def second_layer_early(e):
             dst = staging(e)
             width = dst.shape[1] - C
-            round_w2(dst[:, :width, :], w2_raw[e, 0], nc.vector.tensor_copy if e >= E - VECTOR_ROUNDS else nc.scalar.copy)
+            round_w2(dst[:, :width, :], w2_raw[e, 0], nc.vector.tensor_copy if e >= E - 3 else nc.scalar.copy)
             kind, bufs = ("whole", 2) if e < WHOLE else ("first", E - WHOLE)
             words = stage.tile([P, width + C], U32, name="words_" + kind, align_bytes=64, bufs=bufs)
             scales = stage.tile([P, width + C], U8, name="scales_" + kind, align_bytes=64, bufs=bufs)
@@ -160,72 +181,97 @@ def tile_moe_pkd_mlp_silu_kernel(tc, x_words, x_scales, w1, w2, gate, offs, pos1
             h_mx[e] = (words[:, width:], scales[:, width:])
             for rt in range(width // P):
                 ch = slice(rt * P, (rt + 1) * P)
-                multiply_w2(e, rt, words[:, ch], scales[:, ch], EARLY_GROUPS)
+                multiply_w2(e, rt, words[:, ch], scales[:, ch], whole_groups if rt else early_groups)
 
         def second_layer_late(rt):
-            late = raw.tile([P, len(split) * P, PACK], BF16, name="late_bf16", tag="big", bufs=E, align_bytes=64)
-            late_staging[rt] = late
-            for group in LATE_GROUPS[rt]:
+            late_staging[rt] = []
+            for group in late_groups:
                 width = len(group) * P
-                c0 = (group[0] - WHOLE) * P
+                late = raw.tile([P, width, PACK], BF16, name="late_bf16", tag="big", bufs=E, align_bytes=64)
+                late_staging[rt].append(late)
                 for i, e in enumerate(group):
-                    round_w2(late[:, c0 + i * P : c0 + (i + 1) * P, :], w2_raw[e, rt], nc.scalar.copy)
-                words = stage.tile([P, width], U32, name="words_late", align_bytes=64, bufs=4)
-                scales = stage.tile([P, width], U8, name="scales_late", align_bytes=64, bufs=4)
-                nc.vector.quantize_mx(words[:].bitcast(FP8X4), scales[:], late[:, c0 : c0 + width, :].rearrange("p c j -> p (c j)"))
+                    round_w2(late[:, i * P : (i + 1) * P, :], w2_raw[e, rt], nc.scalar.copy)
+                if group == late_groups[-1]:
+                    empty_bank(rt, late_groups[0])
+                words = stage.tile([P, width], U32, name="words_late", align_bytes=64, bufs=3)
+                scales = stage.tile([P, width], U8, name="scales_late", align_bytes=64, bufs=3)
+                nc.vector.quantize_mx(words[:].bitcast(FP8X4), scales[:], late[:].rearrange("p c j -> p (c j)"))
                 for i, e in enumerate(group):
                     ch = slice(i * P, (i + 1) * P)
-                    multiply_w2(e, rt, words[:, ch], scales[:, ch], LATE_GROUPS[rt])
+                    multiply_w2(e, rt, words[:, ch], scales[:, ch], late_groups)
 
-        def combine(rt):
-            terms = [stage.tile([P, T], F32, name="term%d" % r, bufs=2)[:] for r in range(TOP - 1)]
-            halves = [slice(0, T // 2), slice(T // 2, T)]
-            last = rt + 1 == ROW_TILES
-            if last:
-                terms.append(stage.tile([P, T], F32, name="last_term", bufs=1)[:])
-                total = terms[0]
-            else:
-                spent = late_staging[rt + 1][:].rearrange("p c j -> p (c j)").bitcast(F32)
-                terms.append(spent[:, :T])
-                total = spent[:, spent.shape[1] - T :]
+        def products(rt, last_term):
+            terms = [stage.tile([P, T], F32, name="term%d" % r, bufs=2)[:] for r in range(TOP - 1)] + [last_term]
             for r in range(TOP):
-                nc.vector.tensor_tensor(terms[r], y[rt][:].indirect(pos_sb[r][:]), gate_sb[rt][:, r, :], MULT)
+                nc.vector.tensor_tensor(terms[r], y[rt][:].indirect(pos_sb[r][:]), gate_sb[:, r, :], MULT)
+            return terms
+
+        def add_turned(terms):
+            bank = psum.tile([P, T], F32, name="a_bank", bufs=3)
+            for b in range(T // P):
+                toks = slice(b * P, (b + 1) * P)
+                for r in range(TOP):
+                    nc.tensor.matmul(bank[:, toks], terms[r][:, toks], identity[:], start=r == 0, stop=r == TOP - 1, is_transpose=True)
+            return bank
+
+        def turn_back(rt, bank, turned):
+            nc.scalar.copy(turned, bank[:])
+            back = psum.tile([P, T], F32, name="a_bank", bufs=3)
+            for b in range(T // P):
+                toks = slice(b * P, (b + 1) * P)
+                nc.tensor.transpose(back[:, toks], turned[:, toks], identity[:])
+            total = raw.tile([P, T], F32, name="total", tag="big", bufs=E, align_bytes=64)
+            nc.scalar.copy(total[:], back[:])
+            nc.sync.dma_start(out[rt * P : (rt + 1) * P, :], total[:])
+
+        def add_on_vector(rt, terms):
+            halves = [slice(0, T // 2), slice(T // 2, T)]
+            total = terms[0]
             for toks in halves:
                 nc.vector.tensor_tensor(total[:, toks], terms[0][:, toks], terms[1][:, toks], ADD)
             for toks in halves:
                 nc.vector.tensor_tensor(total[:, toks], total[:, toks], terms[2][:, toks], ADD)
-                if last:
-                    nc.sync.dma_start(out[rt * P : (rt + 1) * P, toks], total[:, toks])
-            if not last:
-                nc.sync.dma_start(out[rt * P : (rt + 1) * P, :], total)
+                nc.sync.dma_start(out[rt * P : (rt + 1) * P, toks], total[:, toks])
 
+        def spent(rt, i):
+            return late_staging[rt][i][:].rearrange("p c j -> p (c j)").bitcast(F32)
+
+        load_gate()
         load_tokens()
-        for step in range(E + LAG):
-            if step < E:
-                load_w1(step)
+        for step in range(E):
+            load_w1(step)
             if step == 4:
                 for r, pos in enumerate((pos1, pos2, pos3)):
                     nc.sync.dma_start(pos_sb[r][:], pos)
-            if 0 <= step - LAG < WHOLE:
-                load_w2_whole(step - LAG)
-            elif step - LAG >= WHOLE:
-                load_w2_first_part(step - LAG)
+            if step in whole_after:
+                load_w2_whole(whole_after[step])
+        for e in range(WHOLE, E):
+            load_w2_first_part(e)
+        for rt in range(1, ROW_TILES):
+            load_w2_late_parts(rt)
 
-        for step in range(E + LAG):
-            if step < E:
-                if step % GATHER_EXPERTS == 0:
-                    gather_tokens(step)
-                first_layer(step)
-            if step >= LAG:
-                second_layer_early(step - LAG)
-            if 1 <= step <= E:
-                activate(step - 1)
-
-        for rt in range(ROW_TILES):
-            if rt > 0:
-                load_w2_late_parts(rt)
-            load_gate(rt)
-        for rt in range(ROW_TILES):
-            if rt + 1 < ROW_TILES:
-                second_layer_late(rt + 1)
-            combine(rt)
+        spread_gate()
+        for e0 in range(0, E, GATHER_EXPERTS):
+            gather_tokens(e0)
+        for step in range(E):
+            first_layer(step)
+            if step == SCALAR_ALONE - 1:
+                for e in range(step):
+                    activate(e)
+            if step in whole_after:
+                second_layer_early(whole_after[step])
+                if step - 1 not in whole_after and step >= SCALAR_ALONE:
+                    activate(step - 1)
+                activate(step)
+        for e in range(WHOLE, E):
+            second_layer_early(e)
+            if e == E - 4:
+                activate(E - 1)
+        second_layer_late(1)
+        sums = add_turned(products(0, spent(1, 1)))
+        second_layer_late(2)
+        turn_back(0, sums, spent(2, 0)[:, :T])
+        sums = add_turned(products(1, spent(2, 1)))
+        turn_back(1, sums, spent(2, 0)[:, T:])
+        last_term = raw.tile([P, T], F32, name="last_term", tag="big", bufs=E, align_bytes=64)
+        add_on_vector(2, products(2, last_term[:]))

@@ -49,7 +49,7 @@ def tile_moe_pkd_mlp_silu_kernel(tc, x_words, x_scales, w1, w2, gate, offs, pos1
         y = [keep.tile([P, SLOTS], F32, name="y%d" % r, align_bytes=64) for r in range(ROW_TILES)]
         identity = keep.tile([P, P], F32, name="identity", align_bytes=64)
         warm = keep.tile([P, 1], F32, name="warm")
-        gate_cols = keep.tile([P, TOP, T // P], F32, name="gate_cols", align_bytes=64)
+        gate_cols = keep.tile([P, TOP, 8], F32, name="gate_cols", align_bytes=64)
         gate_sb = keep.tile([P, TOP, T], F32, name="gate_sb", align_bytes=64)
 
         w1_raw, w2_raw, banks, h_mx, a_banks, late_staging = {}, {}, {}, {}, {}, {}
@@ -58,11 +58,13 @@ def tile_moe_pkd_mlp_silu_kernel(tc, x_words, x_scales, w1, w2, gate, offs, pos1
             nc.vector.memset(tok_scales[:], 0)
             nc.sync.dma_start(offs_sb[:], offs)
             nc.sync.dma_start(tok_words[:], x_words[0].rearrange("p t r -> p (t r)").bitcast(I32))
+
+        def load_token_scales():
             for q in range(4):
                 nc.sync.dma_start(tok_scales[32 * q : 32 * q + 4, :], x_scales[0, 4 * q : 4 * q + 4, :].bitcast(I32))
 
         def load_gate():
-            nc.sync.dma_start(gate_cols[:], gate[:, 0, :].rearrange("r (p c) -> p r c", p=P))
+            nc.sync.dma_start(gate_cols[:, :, : T // P], gate[:, 0, :].rearrange("r (p c) -> p r c", p=P))
 
         def spread_gate():
             make_identity(nc, identity[:])
@@ -240,13 +242,14 @@ def tile_moe_pkd_mlp_silu_kernel(tc, x_words, x_scales, w1, w2, gate, offs, pos1
         load_tokens()
         for step in range(E):
             load_w1(step)
-            if step == 4:
-                for r, pos in enumerate((pos1, pos2, pos3)):
-                    nc.sync.dma_start(pos_sb[r][:], pos)
+            if step == 0:
+                load_token_scales()
             if step in whole_after:
                 load_w2_whole(whole_after[step])
         for e in range(WHOLE, E):
             load_w2_first_part(e)
+        for r, pos in enumerate((pos1, pos2, pos3)):
+            nc.sync.dma_start(pos_sb[r][:], pos)
         for rt in range(1, ROW_TILES):
             load_w2_late_parts(rt)
 

@@ -26,6 +26,7 @@ SCALAR_ALONE = 3
 WHOLE = 6
 BANK = 4
 GATHER_EXPERTS = 3
+TURNED = 256
 
 
 def tile_moe_pkd_mlp_silu_kernel(tc, x_words, x_scales, w1, w2, gate, offs, pos1, pos2, pos3, out):
@@ -46,7 +47,7 @@ def tile_moe_pkd_mlp_silu_kernel(tc, x_words, x_scales, w1, w2, gate, offs, pos1
         tok_scales = keep.tile([P, T // 4], I32, name="tok_scales", align_bytes=64)
         slot_words = keep.tile([P, SLOTS], U32, name="slot_words", align_bytes=64)
         slot_scales = keep.tile([P, SLOTS], U8, name="slot_scales", align_bytes=64)
-        y = [keep.tile([P, SLOTS], F32, name="y%d" % r, align_bytes=64) for r in range(ROW_TILES)]
+        y = [keep.tile([P, SLOTS + (T if r else 0)], F32, name="y%d" % r, align_bytes=64) for r in range(ROW_TILES)]
         identity = keep.tile([P, P], F32, name="identity", align_bytes=64)
         warm = keep.tile([P, 1], F32, name="warm")
         gate_cols = keep.tile([P, TOP, 8], F32, name="gate_cols", align_bytes=64)
@@ -97,7 +98,7 @@ def tile_moe_pkd_mlp_silu_kernel(tc, x_words, x_scales, w1, w2, gate, offs, pos1
                 tile = raw.tile([P, len(group), PACK, P], F32, name="w2_late", tag="big", bufs=E, align_bytes=64)
                 for i, e in enumerate(group):
                     if e == E - 1:
-                        dest = y[rt][:, WHOLE * C : (WHOLE + BANK) * C].rearrange("p (j n) -> p j n", j=PACK)
+                        dest = y[rt][:, (WHOLE + BANK - 1) * C : SLOTS + P].rearrange("p (j n) -> p j n", j=PACK)
                     else:
                         dest = tile[:, i]
                     load_w2_part(e, rt, dest)
@@ -202,11 +203,15 @@ def tile_moe_pkd_mlp_silu_kernel(tc, x_words, x_scales, w1, w2, gate, offs, pos1
                     ch = slice(i * P, (i + 1) * P)
                     multiply_w2(e, rt, words[:, ch], scales[:, ch], late_groups)
 
-        def products(rt, last_term):
-            terms = [stage.tile([P, T], F32, name="term%d" % r, bufs=2)[:] for r in range(TOP - 1)] + [last_term]
+        def new_terms(last_term):
+            return [stage.tile([P, T], F32, name="term%d" % r, bufs=2)[:] for r in range(TOP - 1)] + [last_term]
+
+        def products(rt, terms, first, count):
+            toks = slice(first, first + count)
             for r in range(TOP):
-                nc.vector.tensor_tensor(terms[r], y[rt][:].indirect(pos_sb[r][:]), gate_sb[:, r, :], MULT)
-            return terms
+                entries = pos_sb[r][:, first // 16 : (first + count) // 16]
+                nc.vector.tensor_tensor(terms[r][:, toks], y[rt][:].indirect(entries), gate_sb[:, r, toks], MULT)
+            return [term[:, toks] for term in terms]
 
         def add_turned(terms):
             bank = psum.tile([P, T], F32, name="a_bank", bufs=3)
@@ -216,24 +221,29 @@ def tile_moe_pkd_mlp_silu_kernel(tc, x_words, x_scales, w1, w2, gate, offs, pos1
                     nc.tensor.matmul(bank[:, toks], terms[r][:, toks], identity[:], start=r == 0, stop=r == TOP - 1, is_transpose=True)
             return bank
 
-        def turn_back(rt, bank, turned):
-            nc.scalar.copy(turned, bank[:])
-            back = psum.tile([P, T], F32, name="a_bank", bufs=3)
-            for b in range(T // P):
+        def add_turned_apart(terms):
+            sums = []
+            for b in range(terms[0].shape[1] // P):
+                tag, bufs = ("a_bank", 3) if b % 2 else ("y_bank", 5)
+                sums.append(psum.tile([P, P], F32, name="block_sum", tag=tag, bufs=bufs))
+            for r in range(TOP):
+                for b, bank in enumerate(sums):
+                    nc.tensor.matmul(bank[:], terms[r][:, b * P : (b + 1) * P], identity[:], start=r == 0, stop=r == TOP - 1, is_transpose=True)
+            return sums
+
+        def turn_back(rt, sums, turned):
+            count = turned.shape[1]
+            width = count // len(sums)
+            for b, bank in enumerate(sums):
+                nc.scalar.copy(turned[:, b * width : (b + 1) * width], bank[:])
+            back = psum.tile([P, count], F32, name="back", tag="y_bank", bufs=5)
+            for b in range(count // P):
                 toks = slice(b * P, (b + 1) * P)
                 nc.tensor.transpose(back[:, toks], turned[:, toks], identity[:])
-            total = raw.tile([P, T], F32, name="total", tag="big", bufs=E, align_bytes=64)
-            nc.scalar.copy(total[:], back[:])
-            nc.sync.dma_start(out[rt * P : (rt + 1) * P, :], total[:])
-
-        def add_on_vector(rt, terms):
-            halves = [slice(0, T // 2), slice(T // 2, T)]
-            total = terms[0]
-            for toks in halves:
-                nc.vector.tensor_tensor(total[:, toks], terms[0][:, toks], terms[1][:, toks], ADD)
-            for toks in halves:
-                nc.vector.tensor_tensor(total[:, toks], total[:, toks], terms[2][:, toks], ADD)
-                nc.sync.dma_start(out[rt * P : (rt + 1) * P, toks], total[:, toks])
+            total = y[0][:, rt * T : rt * T + count]
+            nc.scalar.copy(total, back[:])
+            queue = nc.scalar if rt else nc.sync
+            queue.dma_start(out[rt * P : (rt + 1) * P, :count], total)
 
         def spent(rt, i):
             return late_staging[rt][i][:].rearrange("p c j -> p (c j)").bitcast(F32)
@@ -271,10 +281,14 @@ def tile_moe_pkd_mlp_silu_kernel(tc, x_words, x_scales, w1, w2, gate, offs, pos1
             if e == E - 4:
                 activate(E - 1)
         second_layer_late(1)
-        sums = add_turned(products(0, spent(1, 1)))
+        sums = add_turned(products(0, new_terms(y[1][:, SLOTS:]), 0, T))
         second_layer_late(2)
-        turn_back(0, sums, spent(2, 0)[:, :T])
-        sums = add_turned(products(1, spent(2, 1)))
-        turn_back(1, sums, spent(2, 0)[:, T:])
-        last_term = raw.tile([P, T], F32, name="last_term", tag="big", bufs=E, align_bytes=64)
-        add_on_vector(2, products(2, last_term[:]))
+        turn_back(0, [sums], spent(2, 0)[:, T:])
+        sums = add_turned_apart(products(1, new_terms(y[2][:, SLOTS:]), 0, T))
+        turn_back(1, sums, spent(2, 0)[:, :T])
+        terms = new_terms(spent(1, 1))
+        turn_back(2, add_turned_apart(products(2, terms, 0, TURNED)), spent(1, 0)[:, :TURNED])
+        first, second, third = products(2, terms, TURNED, T - TURNED)
+        nc.vector.tensor_tensor(first, first, second, ADD)
+        nc.vector.tensor_tensor(first, first, third, ADD)
+        nc.sync.dma_start(out[2 * P :, TURNED:], first)

@@ -23,7 +23,7 @@ P = 128
 PACK = 4
 ROW_TILES = N // P
 SCALAR_ALONE = 3
-WHOLE = 6
+WHOLE = 5
 BANK = 4
 GATHER_EXPERTS = 3
 TURNED = 256
@@ -32,9 +32,9 @@ TURNED = 256
 def tile_moe_pkd_mlp_silu_kernel(tc, x_words, x_scales, w1, w2, gate, offs, pos1, pos2, pos3, out):
     nc = tc.nc
     early_groups = [(0, 1, 2, 3), (4, 5, 6, 7), (8, 9, 10), (11,)]
-    whole_groups = [(0, 1, 2, 3), (4, 5)]
-    late_groups = [(6, 7, 8, 9), (10, 11)]
-    whole_after = {max(e + 2, 2 * e): e for e in range(WHOLE)}
+    whole_groups = [(0, 1, 2, 3), (4,)]
+    late_groups = [(5, 6, 7, 8), (9, 10), (11,)]
+    whole_after = {2 * e + 2: e for e in range(WHOLE)}
     with ExitStack() as ctx:
         keep = ctx.enter_context(tc.tile_pool(name="keep", bufs=1))
         raw = ctx.enter_context(tc.tile_pool(name="raw", bufs=1))
@@ -95,10 +95,11 @@ def tile_moe_pkd_mlp_silu_kernel(tc, x_words, x_scales, w1, w2, gate, offs, pos1
 
         def load_w2_late_parts(rt):
             for group in late_groups:
-                tile = raw.tile([P, len(group), PACK, P], F32, name="w2_late", tag="big", bufs=E, align_bytes=64)
+                if group != (E - 1,):
+                    tile = raw.tile([P, len(group), PACK, P], F32, name="w2_late", tag="big", bufs=E, align_bytes=64)
                 for i, e in enumerate(group):
                     if e == E - 1:
-                        dest = y[rt][:, (WHOLE + BANK - 1) * C : SLOTS + P].rearrange("p (j n) -> p j n", j=PACK)
+                        dest = y[rt][:, (WHOLE + BANK - 1) * C :].rearrange("p (j n) -> p j n", j=PACK)[:, :, :P]
                     else:
                         dest = tile[:, i]
                     load_w2_part(e, rt, dest)
@@ -137,6 +138,8 @@ def tile_moe_pkd_mlp_silu_kernel(tc, x_words, x_scales, w1, w2, gate, offs, pos1
             width = (N if e < WHOLE else P) + C
             if e < SCALAR_ALONE - 1:
                 flat = w1_raw[SCALAR_ALONE - 1][:].rearrange("p j c -> p (j c)").bitcast(BF16)[:, e * PACK * H :]
+            elif e == SCALAR_ALONE:
+                flat = w1_raw[e][:].rearrange("p j c -> p (j c)").bitcast(BF16)
             elif e in whole_after:
                 flat = w2_raw[whole_after[e], 0].rearrange("p j n -> p (j n)").bitcast(BF16)
             elif e + 1 in whole_after:
@@ -166,11 +169,11 @@ def tile_moe_pkd_mlp_silu_kernel(tc, x_words, x_scales, w1, w2, gate, offs, pos1
                 start=True,
                 stop=True,
             )
-            if e == group[-1] and group != late_groups[0]:
+            if e == group[-1] and group not in late_groups[:-1]:
                 empty_bank(rt, group)
 
         def empty_bank(rt, group):
-            copy = nc.vector.tensor_copy if group == (E - 1,) else nc.scalar.copy
+            copy = nc.vector.tensor_copy if (rt, group) == (0, (E - 1,)) else nc.scalar.copy
             copy(y[rt][:, group[0] * C : (group[-1] + 1) * C], banks[rt, group][:])
 
         def second_layer_early(e):
@@ -195,7 +198,8 @@ def tile_moe_pkd_mlp_silu_kernel(tc, x_words, x_scales, w1, w2, gate, offs, pos1
                 for i, e in enumerate(group):
                     round_w2(late[:, i * P : (i + 1) * P, :], w2_raw[e, rt], nc.scalar.copy)
                 if group == late_groups[-1]:
-                    empty_bank(rt, late_groups[0])
+                    for held in late_groups[:-1]:
+                        empty_bank(rt, held)
                 words = stage.tile([P, width], U32, name="words_late", align_bytes=64, bufs=3)
                 scales = stage.tile([P, width], U8, name="scales_late", align_bytes=64, bufs=3)
                 nc.vector.quantize_mx(words[:].bitcast(FP8X4), scales[:], late[:].rearrange("p c j -> p (c j)"))

@@ -49,7 +49,6 @@ def tile_moe_pkd_mlp_silu_kernel(tc, x_words, x_scales, w1, w2, gate, offs, pos1
         slot_scales = keep.tile([P, SLOTS], U8, name="slot_scales", align_bytes=64)
         y = [keep.tile([P, SLOTS + (T if r else 0)], F32, name="y%d" % r, align_bytes=64) for r in range(ROW_TILES)]
         identity = keep.tile([P, P], F32, name="identity", align_bytes=64)
-        warm = keep.tile([P, 1], F32, name="warm")
         gate_cols = keep.tile([P, TOP, 8], F32, name="gate_cols", align_bytes=64)
         gate_sb = keep.tile([P, TOP, T], F32, name="gate_sb", align_bytes=64)
 
@@ -69,7 +68,6 @@ def tile_moe_pkd_mlp_silu_kernel(tc, x_words, x_scales, w1, w2, gate, offs, pos1
 
         def spread_gate():
             make_identity(nc, identity[:])
-            nc.scalar.activation(warm[:], identity[:, 0:1], SILU)
             for r in range(TOP):
                 bank = psum.tile([P, T], F32, name="y_bank", bufs=5)
                 for c in range(T // P):

@@ -151,7 +151,7 @@ def tile_moe_pkd_mlp_silu_kernel(tc, x_words, x_scales, w1, w2, gate, offs, pos1
             nc.scalar.activation(dst[:, dst.shape[1] - C :, :], a_banks[e][:].rearrange("p t c -> p c t"), SILU)
 
         def round_w2(dst, src, copy):
-            copy(dst.rearrange("p (c i) j -> p c j i", i=4), src.rearrange("p j (c i) -> p c j i", i=4))
+            copy(dst.rearrange("p (c i) j -> p c j i", i=2), src.rearrange("p j (c i) -> p c j i", i=2))
 
         def multiply_w2(e, rt, words, scales, groups):
             group = [g for g in groups if e in g][0]

@@ -18,53 +18,127 @@ FP8X4 = mybir.dt.float8_e4m3fn_x4
 MULT = mybir.AluOpType.mult
 ADD = mybir.AluOpType.add
 SILU = mybir.ActivationFunctionType.Silu
+COPY = mybir.ActivationFunctionType.Copy
 
 P = 128
 PACK = 4
 ROW_TILES = N // P
-SCALAR_ALONE = 3
 WHOLE = 5
-BANK = 4
+LAG = 2
+SCALAR_HEAD = 3
 GATHER_EXPERTS = 3
-TURNED = 256
+HALF = T // 2
+CARRIER = 10
+EARLY_PARTS = 3
 
 
 def tile_moe_pkd_mlp_silu_kernel(tc, x_words, x_scales, w1, w2, gate, offs, pos1, pos2, pos3, out):
     nc = tc.nc
-    early_groups = [(0, 1, 2, 3), (4, 5, 6, 7), (8, 9, 10), (11,)]
-    whole_groups = [(0, 1, 2, 3), (4,)]
-    late_groups = [(5, 6, 7, 8), (9, 10), (11,)]
-    whole_after = {2 * e + 2: e for e in range(WHOLE)}
     with ExitStack() as ctx:
         keep = ctx.enter_context(tc.tile_pool(name="keep", bufs=1))
-        raw = ctx.enter_context(tc.tile_pool(name="raw", bufs=1))
-        stage = ctx.enter_context(tc.tile_pool(name="stage", bufs=3))
+        stage = ctx.enter_context(tc.tile_pool(name="stage", bufs=2))
         psum = ctx.enter_context(tc.psum_pool(name="psum", bufs=2))
 
         offs_sb = keep.tile([P, SLOTS // 16], U16, name="offs_sb")
         pos_sb = [keep.tile([P, T // 16], U16, name="pos_sb%d" % r) for r in range(TOP)]
         tok_words = keep.tile([P, T], I32, name="tok_words", align_bytes=64)
         tok_scales = keep.tile([P, T // 4], I32, name="tok_scales", align_bytes=64)
+        scale_rows = keep.tile([P, 4, T // 4], I32, name="scale_rows", align_bytes=64)
         slot_words = keep.tile([P, SLOTS], U32, name="slot_words", align_bytes=64)
         slot_scales = keep.tile([P, SLOTS], U8, name="slot_scales", align_bytes=64)
-        y = [keep.tile([P, SLOTS + (T if r else 0)], F32, name="y%d" % r, align_bytes=64) for r in range(ROW_TILES)]
+        y = [keep.tile([P, SLOTS + (T if rt else 0)], F32, name="y%d" % rt, align_bytes=64) for rt in range(ROW_TILES)]
         identity = keep.tile([P, P], F32, name="identity", align_bytes=64)
         gate_cols = keep.tile([P, TOP, 8], F32, name="gate_cols", align_bytes=64)
         gate_sb = keep.tile([P, TOP, T], F32, name="gate_sb", align_bytes=64)
+        w1_head = keep.tile([P, SCALAR_HEAD * PACK * H], F32, name="w1_head", align_bytes=64)
+        w1_raw = [w1_head[:, place * PACK * H : (place + 1) * PACK * H] for place in (2, 0, 1)]
+        w1_raw.extend([keep.tile([P, PACK * H], F32, name="w1_raw%d" % e, align_bytes=64)[:] for e in range(SCALAR_HEAD, E)])
+        w2_room = [keep.tile([P, PACK * H], F32, name="w2_room%d" % e, align_bytes=64) for e in range(WHOLE - 2)]
+        w2_raw = [room[:, PACK * (H - N) :] for room in w2_room]
+        w2_last = keep.tile([P, 2 * PACK * N], F32, name="w2_last", align_bytes=64)
+        w2_raw.extend([w2_last[:, : PACK * N], w2_last[:, PACK * N :]])
+        rounded = keep.tile([P, PACK * H], BF16, name="rounded", align_bytes=64)
+        head = [keep.tile([P, PACK * H], BF16, name="head%d" % e, align_bytes=64) for e in range(SCALAR_HEAD - 1)]
 
-        w1_raw, w2_raw, banks, h_mx, a_banks, late_staging = {}, {}, {}, {}, {}, {}
+        a_banks, y_banks, h_mx = {}, {}, {}
+        groups = [(0,), (1, 2, 3, 4), (5, 6, 7, 8), (9, 10), (11,)]
+        late_groups = groups[2:]
+        part = PACK * P
+        carried = w2_last[:, PACK * N - 5 * part // 2 : PACK * N + 3 * part // 2].bitcast(BF16)
+        spent_head = w1_head[:].bitcast(BF16)
 
-        def load_tokens():
-            nc.vector.memset(tok_scales[:], 0)
-            nc.sync.dma_start(offs_sb[:], offs)
-            nc.sync.dma_start(tok_words[:], x_words[0].rearrange("p t r -> p (t r)").bitcast(I32))
+        def part_raw(rt, e):
+            if rt and e == E - 1:
+                return y[rt][:, 8 * C :].rearrange("p (j n) -> p j n", j=PACK)[:, :, :P]
+            place = [0, 8, 16][rt] + e - WHOLE
+            if rt == 2 and e > 8:
+                place = e + 5
+            return w1_raw[SCALAR_HEAD + place // 4][:, place % 4 * part : (place % 4 + 1) * part].rearrange("p (j n) -> p j n", j=PACK)
 
-        def load_token_scales():
-            for q in range(4):
-                nc.sync.dma_start(tok_scales[32 * q : 32 * q + 4, :], x_scales[0, 4 * q : 4 * q + 4, :].bitcast(I32))
+        def late_staging(rt, group):
+            first = [0, 10, 17][rt] + (group[0] - WHOLE) * (1 if rt or group[0] < 10 else 2) - (4 if rt == 0 and group[0] > 10 else 0)
+            width = len(group) * (2 if rt == 0 and group[0] > 8 else 1)
+            return spent_head[:, first * part : (first + width) * part]
 
-        def load_gate():
-            nc.sync.dma_start(gate_cols[:, :, : T // P], gate[:, 0, :].rearrange("r (p c) -> p r c", p=P))
+        def part_staging(rt, e):
+            group = [g for g in late_groups if e in g][0]
+            stride = 2 if rt == 0 and e > 8 else 1
+            place = (e - group[0]) * stride
+            return late_staging(rt, group)[:, place * part : (place + 1) * part]
+
+        def joint_staging(step):
+            rider = step - LAG - 1
+            if step == CARRIER:
+                return carried
+            if rider >= LAG:
+                return w2_room[rider - LAG][:].bitcast(BF16)
+            first = (3 - 2 * rider) * PACK * H // 2
+            return w1_head[:, first : first + PACK * H].bitcast(BF16)
+
+        def halves(step, joint):
+            width = joint.shape[1] // 2
+            first, second = joint[:, :width], joint[:, width:]
+            return (second, first) if step == LAG + 1 else (first, second)
+
+        def w1_staging(e):
+            if 0 <= e - LAG - 1 < WHOLE or e == CARRIER:
+                return halves(e, joint_staging(e))[0]
+            return head[e % 2][:] if e < SCALAR_HEAD - 1 or e > WHOLE + LAG else rounded[:]
+
+        def second_staging(e):
+            return halves(e + LAG + 1, joint_staging(e + LAG + 1))[1]
+
+        def h_staging(e):
+            if e < WHOLE:
+                return second_staging(e)[:, PACK * N :]
+            if e < 9:
+                return carried[:, (e - 1) * part : e * part]
+            group = [g for g in late_groups if e in g][0]
+            place = 2 * (e - group[0]) + 1
+            return late_staging(0, group)[:, place * part : (place + 1) * part]
+
+        def term(rt, r):
+            if r == TOP - 1 and rt < ROW_TILES - 1:
+                return y[rt + 1][:, SLOTS:]
+            place = 2 * rt + r
+            return w2_room[place // 4][:, place % 4 * T : (place % 4 + 1) * T]
+
+        def load_w1(e):
+            nc.sync.dma_start(w1_raw[e].rearrange("p (j c) -> p j c", j=PACK), w1[e].rearrange("(p j) c -> p j c", j=PACK))
+
+        def load_w2(e):
+            nc.sync.dma_start(w2_raw[e].rearrange("p (j n) -> p j n", j=PACK), w2[e].rearrange("(p j) n -> p j n", j=PACK))
+
+        def load_late():
+            for rt in range(ROW_TILES):
+                for e in range(WHOLE, E):
+                    if (rt, e) == (0, WHOLE + EARLY_PARTS):
+                        load_w1(E - 1)
+                    rows = w2[e].rearrange("(p j) n -> p j n", j=PACK)
+                    nc.sync.dma_start(part_raw(rt, e), rows[:, :, rt * P : (rt + 1) * P])
+                if rt == 0:
+                    for r, pos in enumerate((pos1, pos2, pos3)):
+                        nc.sync.dma_start(pos_sb[r][:], pos)
 
         def spread_gate():
             make_identity(nc, identity[:])
@@ -74,55 +148,33 @@ def tile_moe_pkd_mlp_silu_kernel(tc, x_words, x_scales, w1, w2, gate, offs, pos1
                     nc.tensor.transpose(bank[:, c * P : (c + 1) * P], gate_cols[:, r, c : c + 1].to_broadcast([P, P]), identity[:])
                 nc.scalar.copy(gate_sb[:, r, :].rearrange("n (p c) -> n p c", p=P), bank[:].rearrange("n (c p) -> n p c", p=P))
 
-        def load_w1(e):
-            w1_raw[e] = raw.tile([P, PACK, H], F32, name="w1_raw", tag="big", bufs=E, align_bytes=64)
-            nc.sync.dma_start(w1_raw[e][:], w1[e].rearrange("(p j) c -> p j c", j=PACK))
-
-        def load_w2_whole(e):
-            tile = raw.tile([P, PACK, N], F32, name="w2_whole", bufs=WHOLE, align_bytes=64)
-            nc.sync.dma_start(tile[:], w2[e].rearrange("(p j) n -> p j n", j=PACK))
-            w2_raw[e, 0] = tile[:]
-
-        def load_w2_part(e, rt, dest):
-            nc.sync.dma_start(dest, w2[e].rearrange("(p j) n -> p j n", j=PACK)[:, :, rt * P : (rt + 1) * P])
-            w2_raw[e, rt] = dest
-
-        def load_w2_first_part(e):
-            tile = raw.tile([P, PACK, P], F32, name="w2_first", bufs=E - WHOLE, align_bytes=64)
-            load_w2_part(e, 0, tile[:])
-
-        def load_w2_late_parts(rt):
-            for group in late_groups:
-                if group != (E - 1,):
-                    tile = raw.tile([P, len(group), PACK, P], F32, name="w2_late", tag="big", bufs=E, align_bytes=64)
-                for i, e in enumerate(group):
-                    if e == E - 1:
-                        dest = y[rt][:, (WHOLE + BANK - 1) * C :].rearrange("p (j n) -> p j n", j=PACK)[:, :, :P]
-                    else:
-                        dest = tile[:, i]
-                    load_w2_part(e, rt, dest)
-
-        def gather_tokens(e0):
-            cols = slice(e0 * C, (e0 + GATHER_EXPERTS) * C)
-            entries = offs_sb[:, e0 * C // 16 : (e0 + GATHER_EXPERTS) * C // 16]
+        def gather_tokens(batch):
+            width = GATHER_EXPERTS * C // 16
+            entries = offs_sb[:, batch * width : (batch + 1) * width]
+            cols = slice(batch * GATHER_EXPERTS * C, (batch + 1) * GATHER_EXPERTS * C)
             nc.vector.tensor_copy(slot_words[:, cols], tok_words[:].bitcast(U32).indirect(entries))
             nc.vector.tensor_copy(slot_scales[:, cols], tok_scales[:].bitcast(U8).indirect(entries))
 
-        def first_layer(e):
-            grouped = stage.tile([P, PACK * H], BF16, name="w1_bf16", align_bytes=64)
-            dst = grouped[:].rearrange("p (t m j) -> p m j t", t=PACK, j=PACK)
-            src = w1_raw[e][:].rearrange("p j (m t) -> p m j t", t=PACK)
-            copy = nc.scalar.copy if e < SCALAR_ALONE else nc.vector.tensor_copy
+        def round_w1(e):
+            dst = w1_staging(e).rearrange("p (t m j) -> p m j t", t=PACK, j=PACK)
+            src = w1_raw[e].rearrange("p (j m t) -> p m j t", j=PACK, t=PACK)
+            copy = nc.scalar.copy if e < SCALAR_HEAD else nc.vector.tensor_copy
             copy(dst, src)
-            words = stage.tile([P, H], U32, name="w1_words", align_bytes=64)
-            scales = stage.tile([P, H], U8, name="w1_scales", align_bytes=64)
-            nc.vector.quantize_mx(words[:].bitcast(FP8X4), scales[:], grouped[:])
-            a = psum.tile([P, PACK, C], F32, name="a_bank", bufs=3)
+
+        def quantize(src, pool=stage, tag=""):
+            width = src.shape[1] // PACK
+            words = pool.tile([P, width], U32, name="words" + tag, align_bytes=64)
+            scales = pool.tile([P, width], U8, name="scales" + tag, align_bytes=64)
+            nc.vector.quantize_mx(words[:].bitcast(FP8X4), scales[:], src)
+            return words, scales
+
+        def first_product(e, words, scales):
+            a_banks[e] = psum.tile([P, PACK, C], F32, name="a_bank", bufs=3)
             cols = slice(e * C, (e + 1) * C)
             for t in range(PACK):
                 ch = slice(t * P, (t + 1) * P)
                 nc.tensor.matmul_mx(
-                    a[:, t, :],
+                    a_banks[e][:, t, :],
                     lhsT=words[:, ch].bitcast(FP8X4),
                     lhsT_scale=scales[:, ch],
                     rhs=slot_words[:, cols].bitcast(FP8X4),
@@ -130,36 +182,26 @@ def tile_moe_pkd_mlp_silu_kernel(tc, x_words, x_scales, w1, w2, gate, offs, pos1
                     start=True,
                     stop=True,
                 )
-            a_banks[e] = a
-
-        def staging(e):
-            width = (N if e < WHOLE else P) + C
-            if e < SCALAR_ALONE - 1:
-                flat = w1_raw[SCALAR_ALONE - 1][:].rearrange("p j c -> p (j c)").bitcast(BF16)[:, e * PACK * H :]
-            elif e == SCALAR_ALONE:
-                flat = w1_raw[e][:].rearrange("p j c -> p (j c)").bitcast(BF16)
-            elif e in whole_after:
-                flat = w2_raw[whole_after[e], 0].rearrange("p j n -> p (j n)").bitcast(BF16)
-            elif e + 1 in whole_after:
-                flat = w2_raw[whole_after[e + 1], 0].rearrange("p j n -> p (j n)").bitcast(BF16)[:, PACK * (P + C) :]
-            else:
-                flat = w2_raw[E - 4, 0].rearrange("p j n -> p (j n)").bitcast(BF16)
-            return flat[:, : width * PACK].rearrange("p (c j) -> p c j", j=PACK)
 
         def activate(e):
-            dst = staging(e)
-            nc.scalar.activation(dst[:, dst.shape[1] - C :, :], a_banks[e][:].rearrange("p t c -> p c t"), SILU)
+            dst = h_staging(e).rearrange("p (c t) -> p c t", t=PACK)
+            nc.scalar.activation(dst, a_banks[e][:].rearrange("p t c -> p c t"), SILU)
 
         def round_w2(dst, src, copy):
-            copy(dst.rearrange("p (c i) j -> p c j i", i=2), src.rearrange("p j (c i) -> p c j i", i=2))
+            copy(dst.rearrange("p (c i j) -> p c j i", i=2, j=PACK), src.rearrange("p (j c i) -> p c j i", j=PACK, i=2))
 
-        def multiply_w2(e, rt, words, scales, groups):
+        def multiply_w2(e, rt, words, scales):
             group = [g for g in groups if e in g][0]
-            if e == group[0]:
-                banks[rt, group] = psum.tile([P, len(group) * C], F32, name="y_bank", bufs=5)
+            if e == 0 and rt:
+                y_banks[rt, group] = y_banks[0, group, "all"][:, rt * C : (rt + 1) * C]
+            elif e == 0:
+                y_banks[0, group, "all"] = psum.tile([P, ROW_TILES * C], F32, name="y_bank", bufs=5)
+                y_banks[rt, group] = y_banks[0, group, "all"][:, :C]
+            elif e == group[0]:
+                y_banks[rt, group] = psum.tile([P, len(group) * C], F32, name="y_bank", bufs=5)[:]
             place = e - group[0]
             nc.tensor.matmul_mx(
-                banks[rt, group][:, place * C : (place + 1) * C],
+                y_banks[rt, group][:, place * C : (place + 1) * C],
                 lhsT=words.bitcast(FP8X4),
                 lhsT_scale=scales,
                 rhs=h_mx[e][0].bitcast(FP8X4),
@@ -167,130 +209,166 @@ def tile_moe_pkd_mlp_silu_kernel(tc, x_words, x_scales, w1, w2, gate, offs, pos1
                 start=True,
                 stop=True,
             )
-            if e == group[-1] and group not in late_groups[:-1]:
-                empty_bank(rt, group)
 
-        def empty_bank(rt, group):
-            copy = nc.vector.tensor_copy if (rt, group) == (0, (E - 1,)) else nc.scalar.copy
-            copy(y[rt][:, group[0] * C : (group[-1] + 1) * C], banks[rt, group][:])
+        def empty_bank(rt, group, copy=nc.scalar.copy):
+            copy(y[rt][:, group[0] * C : (group[-1] + 1) * C], y_banks[rt, group])
 
-        def second_layer_early(e):
-            dst = staging(e)
-            width = dst.shape[1] - C
-            round_w2(dst[:, :width, :], w2_raw[e, 0], nc.vector.tensor_copy if e >= E - 3 else nc.scalar.copy)
-            kind, bufs = ("whole", 2) if e < WHOLE else ("first", E - WHOLE)
-            words = stage.tile([P, width + C], U32, name="words_" + kind, align_bytes=64, bufs=bufs)
-            scales = stage.tile([P, width + C], U8, name="scales_" + kind, align_bytes=64, bufs=bufs)
-            nc.vector.quantize_mx(words[:].bitcast(FP8X4), scales[:], dst.rearrange("p c j -> p (c j)"))
-            h_mx[e] = (words[:, width:], scales[:, width:])
-            for rt in range(width // P):
+        def second_product(e, words, scales):
+            h_mx[e] = (words[:, N:], scales[:, N:])
+            for rt in range(ROW_TILES):
                 ch = slice(rt * P, (rt + 1) * P)
-                multiply_w2(e, rt, words[:, ch], scales[:, ch], whole_groups if rt else early_groups)
+                multiply_w2(e, rt, words[:, ch], scales[:, ch])
 
-        def second_layer_late(rt):
-            late_staging[rt] = []
+        def round_part(rt, e, copy):
+            dst = part_staging(rt, e).rearrange("p (c i j) -> p c j i", i=2, j=PACK)
+            copy(dst, part_raw(rt, e).rearrange("p j (c i) -> p c j i", i=2))
+
+        def part_products(rt, group):
+            src = late_staging(rt, group)
+            width = src.shape[1] // PACK
+            with_h = width > len(group) * P
+            tag = "kept%d" % group[0] if with_h else "late"
+            words = stage.tile([P, width], U32, name="part_words", tag=tag + "_words", align_bytes=64, bufs=1 if with_h else 3)
+            scales = stage.tile([P, width], U8, name="part_scales", tag=tag + "_scales", align_bytes=64, bufs=1 if with_h else 3)
+            nc.vector.quantize_mx(words[:].bitcast(FP8X4), scales[:], src)
+            for i, e in enumerate(group):
+                first = (2 * i if with_h else i) * P
+                if with_h:
+                    h_mx[e] = (words[:, first + P : first + 2 * P], scales[:, first + P : first + 2 * P])
+                multiply_w2(e, rt, words[:, first : first + P], scales[:, first : first + P])
+
+        def late_row_tile(rt):
             for group in late_groups:
-                width = len(group) * P
-                late = raw.tile([P, width, PACK], BF16, name="late_bf16", tag="big", bufs=E, align_bytes=64)
-                late_staging[rt].append(late)
-                for i, e in enumerate(group):
-                    round_w2(late[:, i * P : (i + 1) * P, :], w2_raw[e, rt], nc.scalar.copy)
+                for e in group:
+                    round_part(rt, e, nc.scalar.copy)
                 if group == late_groups[-1]:
                     for held in late_groups[:-1]:
                         empty_bank(rt, held)
-                words = stage.tile([P, width], U32, name="words_late", align_bytes=64, bufs=3)
-                scales = stage.tile([P, width], U8, name="scales_late", align_bytes=64, bufs=3)
-                nc.vector.quantize_mx(words[:].bitcast(FP8X4), scales[:], late[:].rearrange("p c j -> p (c j)"))
-                for i, e in enumerate(group):
-                    ch = slice(i * P, (i + 1) * P)
-                    multiply_w2(e, rt, words[:, ch], scales[:, ch], late_groups)
+                part_products(rt, group)
+            empty_bank(rt, late_groups[-1])
 
-        def new_terms(last_term):
-            return [stage.tile([P, T], F32, name="term%d" % r, bufs=2)[:] for r in range(TOP - 1)] + [last_term]
+        def entries_of(r, toks):
+            return pos_sb[r][:, toks.start // 16 : toks.stop // 16]
 
-        def products(rt, terms, first, count):
-            toks = slice(first, first + count)
-            for r in range(TOP):
-                entries = pos_sb[r][:, first // 16 : (first + count) // 16]
-                nc.vector.tensor_tensor(terms[r][:, toks], y[rt][:].indirect(entries), gate_sb[:, r, toks], MULT)
-            return [term[:, toks] for term in terms]
+        def fetch_gated(rt, r, toks):
+            nc.vector.tensor_tensor(term(rt, r)[:, toks], y[rt][:].indirect(entries_of(r, toks)), gate_sb[:, r, toks], MULT)
 
-        def add_turned(terms):
+        def fetch(rt, r, toks):
+            nc.scalar.activation(term(rt, r)[:, toks], y[rt][:].indirect(entries_of(r, toks)), COPY)
+
+        def apply_gate(rt, r, toks):
+            nc.vector.tensor_tensor(term(rt, r)[:, toks], term(rt, r)[:, toks], gate_sb[:, r, toks], MULT)
+
+        def add_turned(rt):
             bank = psum.tile([P, T], F32, name="a_bank", bufs=3)
             for b in range(T // P):
                 toks = slice(b * P, (b + 1) * P)
                 for r in range(TOP):
-                    nc.tensor.matmul(bank[:, toks], terms[r][:, toks], identity[:], start=r == 0, stop=r == TOP - 1, is_transpose=True)
-            return bank
+                    nc.tensor.matmul(bank[:, toks], term(rt, r)[:, toks], identity[:], start=r == 0, stop=r == TOP - 1, is_transpose=True)
+            return [bank]
 
-        def add_turned_apart(terms):
+        def add_turned_apart(rt):
             sums = []
-            for b in range(terms[0].shape[1] // P):
+            for b in range(T // P):
                 tag, bufs = ("a_bank", 3) if b % 2 else ("y_bank", 5)
                 sums.append(psum.tile([P, P], F32, name="block_sum", tag=tag, bufs=bufs))
             for r in range(TOP):
                 for b, bank in enumerate(sums):
-                    nc.tensor.matmul(bank[:], terms[r][:, b * P : (b + 1) * P], identity[:], start=r == 0, stop=r == TOP - 1, is_transpose=True)
+                    nc.tensor.matmul(bank[:], term(rt, r)[:, b * P : (b + 1) * P], identity[:], start=r == 0, stop=r == TOP - 1, is_transpose=True)
             return sums
 
-        def turn_back(rt, sums, turned):
-            count = turned.shape[1]
-            width = count // len(sums)
+        def turn_back(rt, sums):
+            turned = spent_head[:, (20 + 2 * (1 - rt)) * part : (22 + 2 * (1 - rt)) * part].bitcast(F32)
+            width = T // len(sums)
             for b, bank in enumerate(sums):
                 nc.scalar.copy(turned[:, b * width : (b + 1) * width], bank[:])
-            back = psum.tile([P, count], F32, name="back", tag="y_bank", bufs=5)
-            for b in range(count // P):
-                toks = slice(b * P, (b + 1) * P)
-                nc.tensor.transpose(back[:, toks], turned[:, toks], identity[:])
-            total = y[0][:, rt * T : rt * T + count]
+            back = psum.tile([P, T], F32, name="back", tag="y_bank", bufs=5)
+            for b in range(T // P):
+                nc.tensor.transpose(back[:, b * P : (b + 1) * P], turned[:, b * P : (b + 1) * P], identity[:])
+            total = y[0][:, rt * T : (rt + 1) * T]
             nc.scalar.copy(total, back[:])
             queue = nc.scalar if rt else nc.sync
-            queue.dma_start(out[rt * P : (rt + 1) * P, :count], total)
+            queue.dma_start(out[rt * P : (rt + 1) * P, :], total)
 
-        def spent(rt, i):
-            return late_staging[rt][i][:].rearrange("p c j -> p (c j)").bitcast(F32)
+        vector, scalar = nc.vector.tensor_copy, nc.scalar.copy
+        everyone, lower, upper = slice(0, T), slice(0, HALF), slice(HALF, T)
 
-        load_gate()
-        load_tokens()
-        for step in range(E):
+        nc.sync.dma_start(gate_cols[:, :, : T // P], gate[:, 0, :].rearrange("r (p c) -> p r c", p=P))
+        nc.vector.memset(tok_scales[:], 0)
+        nc.sync.dma_start(offs_sb[:], offs)
+        nc.sync.dma_start(tok_words[:], x_words[0].rearrange("p t r -> p (t r)").bitcast(I32))
+        for step in range(E - 1):
             load_w1(step)
             if step == 0:
-                load_token_scales()
-            if step in whole_after:
-                load_w2_whole(whole_after[step])
-        for e in range(WHOLE, E):
-            load_w2_first_part(e)
-        for r, pos in enumerate((pos1, pos2, pos3)):
-            nc.sync.dma_start(pos_sb[r][:], pos)
-        for rt in range(1, ROW_TILES):
-            load_w2_late_parts(rt)
+                nc.sync.dma_start(scale_rows[:4], x_scales[0].bitcast(I32).rearrange("(q r) w -> r q w", r=4))
+                for q in range(4):
+                    nc.vector.tensor_copy(tok_scales[32 * q : 32 * q + 4, :], scale_rows[:4, q, :])
+            if 0 <= step - LAG < WHOLE:
+                load_w2(step - LAG)
 
         spread_gate()
-        for e0 in range(0, E, GATHER_EXPERTS):
-            gather_tokens(e0)
+        for batch in range(E // GATHER_EXPERTS):
+            gather_tokens(batch)
         for step in range(E):
-            first_layer(step)
-            if step == SCALAR_ALONE - 1:
+            round_w1(step)
+            if step == SCALAR_HEAD - 1:
                 for e in range(step):
                     activate(e)
-            if step in whole_after:
-                second_layer_early(whole_after[step])
-                if step - 1 not in whole_after and step >= SCALAR_ALONE:
-                    activate(step - 1)
+            if step == 7:
+                load_late()
+            rider = step - LAG - 1
+            if step == CARRIER:
+                words, scales = quantize(carried, keep, "_carried")
+                first_product(step, words[:, :H], scales[:, :H])
+                for e in late_groups[0]:
+                    ch = slice((e - 1) * P, e * P)
+                    h_mx[e] = (words[:, ch], scales[:, ch])
+            elif 0 <= rider < WHOLE:
+                words, scales = quantize(joint_staging(step))
+                own, other = zip(halves(step, words[:]), halves(step, scales[:]))
+                first_product(step, *own)
+                second_product(rider, *other)
+            else:
+                words, scales = quantize(w1_staging(step))
+                first_product(step, words[:], scales[:])
+            done = step - LAG
+            if 0 <= done < WHOLE:
+                round_w2(second_staging(done)[:, : PACK * N], w2_raw[done], scalar)
+            if step == E - 2:
+                for e in range(WHOLE, WHOLE + EARLY_PARTS):
+                    round_part(0, e, scalar)
+            if SCALAR_HEAD - 1 <= step < E - 1:
                 activate(step)
-        for e in range(WHOLE, E):
-            second_layer_early(e)
-            if e == E - 4:
-                activate(E - 1)
-        second_layer_late(1)
-        sums = add_turned(products(0, new_terms(y[1][:, SLOTS:]), 0, T))
-        second_layer_late(2)
-        turn_back(0, [sums], spent(2, 0)[:, T:])
-        sums = add_turned_apart(products(1, new_terms(y[2][:, SLOTS:]), 0, T))
-        turn_back(1, sums, spent(2, 0)[:, :T])
-        terms = new_terms(spent(1, 1))
-        turn_back(2, add_turned_apart(products(2, terms, 0, TURNED)), spent(1, 0)[:, :TURNED])
-        first, second, third = products(2, terms, TURNED, T - TURNED)
-        nc.vector.tensor_tensor(first, first, second, ADD)
-        nc.vector.tensor_tensor(first, first, third, ADD)
-        nc.sync.dma_start(out[2 * P :, TURNED:], first)
+            if rider in (0, WHOLE - 1):
+                for rt in range(ROW_TILES):
+                    empty_bank(rt, groups[rider // 4])
+        for e in (8, 9, 10):
+            round_part(0, e, scalar)
+        activate(E - 1)
+        part_products(0, late_groups[0])
+        round_part(0, 11, vector)
+        empty_bank(0, late_groups[0])
+        part_products(0, late_groups[1])
+        part_products(0, late_groups[2])
+        empty_bank(0, late_groups[1])
+        empty_bank(0, late_groups[2], vector)
+        late_row_tile(1)
+        for r in range(TOP):
+            fetch_gated(0, r, everyone)
+        sums = add_turned(0)
+        late_row_tile(2)
+        for r in range(TOP):
+            fetch_gated(1, r, everyone)
+        fetch(2, 2, lower)
+        turn_back(0, sums)
+        sums = add_turned_apart(1)
+        fetch(2, 2, upper)
+        turn_back(1, sums)
+        for toks in (lower, upper):
+            fetch_gated(2, 0, toks)
+            fetch_gated(2, 1, toks)
+            apply_gate(2, 2, toks)
+            first, second, third = [term(2, r)[:, toks] for r in range(TOP)]
+            nc.vector.tensor_tensor(first, first, second, ADD)
+            nc.vector.tensor_tensor(first, first, third, ADD)
+            nc.sync.dma_start(out[2 * P :, toks], first)

@@ -43,7 +43,6 @@ def tile_moe_pkd_mlp_silu_kernel(tc, x_words, x_scales, w1, w2, gate, offs, pos1
         pos_sb = [keep.tile([P, T // 16], U16, name="pos_sb%d" % r) for r in range(TOP)]
         tok_words = keep.tile([P, T], I32, name="tok_words", align_bytes=64)
         tok_scales = keep.tile([P, T // 4], I32, name="tok_scales", align_bytes=64)
-        scale_rows = keep.tile([P, 4, T // 4], I32, name="scale_rows", align_bytes=64)
         slot_words = keep.tile([P, SLOTS], U32, name="slot_words", align_bytes=64)
         slot_scales = keep.tile([P, SLOTS], U8, name="slot_scales", align_bytes=64)
         y = [keep.tile([P, SLOTS + (T if rt else 0)], F32, name="y%d" % rt, align_bytes=64) for rt in range(ROW_TILES)]
@@ -300,9 +299,8 @@ def tile_moe_pkd_mlp_silu_kernel(tc, x_words, x_scales, w1, w2, gate, offs, pos1
         for step in range(E - 1):
             load_w1(step)
             if step == 0:
-                nc.sync.dma_start(scale_rows[:4], x_scales[0].bitcast(I32).rearrange("(q r) w -> r q w", r=4))
                 for q in range(4):
-                    nc.vector.tensor_copy(tok_scales[32 * q : 32 * q + 4, :], scale_rows[:4, q, :])
+                    nc.sync.dma_start(tok_scales[32 * q : 32 * q + 4, :], x_scales[0, 4 * q : 4 * q + 4, :].bitcast(I32))
             if 0 <= step - LAG < WHOLE:
                 load_w2(step - LAG)
 

@@ -276,11 +276,16 @@ def tile_moe_pkd_mlp_silu_kernel(tc, x_words, x_scales, w1, w2, gate, offs, pos1
                     nc.tensor.matmul(bank[:], term(rt, r)[:, b * P : (b + 1) * P], identity[:], start=r == 0, stop=r == TOP - 1, is_transpose=True)
             return sums
 
-        def turn_back(rt, sums):
-            turned = spent_head[:, (20 + 2 * (1 - rt)) * part : (22 + 2 * (1 - rt)) * part].bitcast(F32)
+        def turned_sums(rt):
+            return late_staging(2, late_groups[0]).bitcast(F32)[:, (1 - rt) * T : (2 - rt) * T]
+
+        def empty_sums(rt, sums):
             width = T // len(sums)
             for b, bank in enumerate(sums):
-                nc.scalar.copy(turned[:, b * width : (b + 1) * width], bank[:])
+                nc.scalar.copy(turned_sums(rt)[:, b * width : (b + 1) * width], bank[:])
+
+        def turn_back(rt):
+            turned = turned_sums(rt)
             back = psum.tile([P, T], F32, name="back", tag="y_bank", bufs=5)
             for b in range(T // P):
                 nc.tensor.transpose(back[:, b * P : (b + 1) * P], turned[:, b * P : (b + 1) * P], identity[:])
@@ -355,13 +360,15 @@ def tile_moe_pkd_mlp_silu_kernel(tc, x_words, x_scales, w1, w2, gate, offs, pos1
             fetch_gated(0, r, everyone)
         sums = add_turned(0)
         late_row_tile(2)
+        empty_sums(0, sums)
+        turn_back(0)
         for r in range(TOP):
             fetch_gated(1, r, everyone)
-        fetch(2, 2, lower)
-        turn_back(0, sums)
         sums = add_turned_apart(1)
+        fetch(2, 2, lower)
+        empty_sums(1, sums)
         fetch(2, 2, upper)
-        turn_back(1, sums)
+        turn_back(1)
         for toks in (lower, upper):
             fetch_gated(2, 0, toks)
             fetch_gated(2, 1, toks)

@@ -29,7 +29,7 @@ SCALAR_HEAD = 3
 GATHER_EXPERTS = 3
 HALF = T // 2
 CARRIER = 10
-EARLY_PARTS = 3
+EARLY_PARTS = 2
 
 
 def tile_moe_pkd_mlp_silu_kernel(tc, x_words, x_scales, w1, w2, gate, offs, pos1, pos2, pos3, out):
@@ -345,10 +345,11 @@ def tile_moe_pkd_mlp_silu_kernel(tc, x_words, x_scales, w1, w2, gate, offs, pos1
             if rider in (0, WHOLE - 1):
                 for rt in range(ROW_TILES):
                     empty_bank(rt, groups[rider // 4])
-        for e in (8, 9, 10):
+        for e in (7, 8, 9):
             round_part(0, e, scalar)
         activate(E - 1)
         part_products(0, late_groups[0])
+        round_part(0, 10, vector)
         round_part(0, 11, vector)
         empty_bank(0, late_groups[0])
         part_products(0, late_groups[1])

from contextlib import ExitStack

import concourse.mybir as mybir
from concourse.masks import make_identity

K, T, E, C, H, N = 512, 512, 12, 128, 512, 384
TOP = 3
SLOTS = E * C
FLOPS = 2 * SLOTS * H * (K + N)

F32 = mybir.dt.float32
BF16 = mybir.dt.bfloat16
I32 = mybir.dt.int32
U32 = mybir.dt.uint32
U16 = mybir.dt.uint16
U8 = mybir.dt.uint8
FP8X4 = mybir.dt.float8_e4m3fn_x4
MULT = mybir.AluOpType.mult
ADD = mybir.AluOpType.add
SILU = mybir.ActivationFunctionType.Silu
COPY = mybir.ActivationFunctionType.Copy

P = 128
PACK = 4
ROW_TILES = N // P
WHOLE = 5
LAG = 2
SCALAR_HEAD = 3
GATHER_EXPERTS = 3
HALF = T // 2
CARRIER = 10
EARLY_PARTS = 2


def tile_moe_pkd_mlp_silu_kernel(tc, x_words, x_scales, w1, w2, gate, offs, pos1, pos2, pos3, out):
    nc = tc.nc
    with ExitStack() as ctx:
        keep = ctx.enter_context(tc.tile_pool(name="keep", bufs=1))
        stage = ctx.enter_context(tc.tile_pool(name="stage", bufs=2))
        psum = ctx.enter_context(tc.psum_pool(name="psum", bufs=2))

        offs_sb = keep.tile([P, SLOTS // 16], U16, name="offs_sb")
        pos_sb = [keep.tile([P, T // 16], U16, name="pos_sb%d" % r) for r in range(TOP)]
        tok_words = keep.tile([P, T], I32, name="tok_words", align_bytes=64)
        tok_scales = keep.tile([P, T // 4], I32, name="tok_scales", align_bytes=64)
        slot_words = keep.tile([P, SLOTS], U32, name="slot_words", align_bytes=64)
        slot_scales = keep.tile([P, SLOTS], U8, name="slot_scales", align_bytes=64)
        y = [keep.tile([P, SLOTS + (T if rt else 0)], F32, name="y%d" % rt, align_bytes=64) for rt in range(ROW_TILES)]
        identity = keep.tile([P, P], F32, name="identity", align_bytes=64)
        gate_cols = keep.tile([P, TOP, 8], F32, name="gate_cols", align_bytes=64)
        gate_sb = keep.tile([P, TOP, T], F32, name="gate_sb", align_bytes=64)
        w1_head = keep.tile([P, SCALAR_HEAD * PACK * H], F32, name="w1_head", align_bytes=64)
        w1_raw = [w1_head[:, place * PACK * H : (place + 1) * PACK * H] for place in (2, 0, 1)]
        w1_raw.extend([keep.tile([P, PACK * H], F32, name="w1_raw%d" % e, align_bytes=64)[:] for e in range(SCALAR_HEAD, E)])
        w2_room = [keep.tile([P, PACK * H], F32, name="w2_room%d" % e, align_bytes=64) for e in range(WHOLE - 2)]
        w2_raw = [room[:, PACK * (H - N) :] for room in w2_room]
        w2_last = keep.tile([P, 2 * PACK * N], F32, name="w2_last", align_bytes=64)
        w2_raw.extend([w2_last[:, : PACK * N], w2_last[:, PACK * N :]])
        rounded = keep.tile([P, PACK * H], BF16, name="rounded", align_bytes=64)
        head = [keep.tile([P, PACK * H], BF16, name="head%d" % e, align_bytes=64) for e in range(SCALAR_HEAD - 1)]

        a_banks, y_banks, h_mx = {}, {}, {}
        groups = [(0,), (1, 2, 3, 4), (5, 6, 7, 8), (9, 10), (11,)]
        late_groups = groups[2:]
        part = PACK * P
        carried = w2_last[:, PACK * N - 5 * part // 2 : PACK * N + 3 * part // 2].bitcast(BF16)
        spent_head = w1_head[:].bitcast(BF16)

        def part_raw(rt, e):
            if rt and e == E - 1:
                return y[rt][:, 8 * C :].rearrange("p (j n) -> p j n", j=PACK)[:, :, :P]
            place = [0, 8, 16][rt] + e - WHOLE
            if rt == 2 and e > 8:
                place = e + 5
            return w1_raw[SCALAR_HEAD + place // 4][:, place % 4 * part : (place % 4 + 1) * part].rearrange("p (j n) -> p j n", j=PACK)

        def late_staging(rt, group):
            first = [0, 10, 17][rt] + (group[0] - WHOLE) * (1 if rt or group[0] < 10 else 2) - (4 if rt == 0 and group[0] > 10 else 0)
            width = len(group) * (2 if rt == 0 and group[0] > 8 else 1)
            return spent_head[:, first * part : (first + width) * part]

        def part_staging(rt, e):
            group = [g for g in late_groups if e in g][0]
            stride = 2 if rt == 0 and e > 8 else 1
            place = (e - group[0]) * stride
            return late_staging(rt, group)[:, place * part : (place + 1) * part]

        def joint_staging(step):
            rider = step - LAG - 1
            if step == CARRIER:
                return carried
            if rider >= LAG:
                return w2_room[rider - LAG][:].bitcast(BF16)
            first = (3 - 2 * rider) * PACK * H // 2
            return w1_head[:, first : first + PACK * H].bitcast(BF16)

        def halves(step, joint):
            width = joint.shape[1] // 2
            first, second = joint[:, :width], joint[:, width:]
            return (second, first) if step == LAG + 1 else (first, second)

        def w1_staging(e):
            if 0 <= e - LAG - 1 < WHOLE or e == CARRIER:
                return halves(e, joint_staging(e))[0]
            return head[e % 2][:] if e < SCALAR_HEAD - 1 or e > WHOLE + LAG else rounded[:]

        def second_staging(e):
            return halves(e + LAG + 1, joint_staging(e + LAG + 1))[1]

        def h_staging(e):
            if e < WHOLE:
                return second_staging(e)[:, PACK * N :]
            if e < 9:
                return carried[:, (e - 1) * part : e * part]
            group = [g for g in late_groups if e in g][0]
            place = 2 * (e - group[0]) + 1
            return late_staging(0, group)[:, place * part : (place + 1) * part]

        def term(rt, r):
            if r == TOP - 1 and rt < ROW_TILES - 1:
                return y[rt + 1][:, SLOTS:]
            place = 2 * rt + r
            return w2_room[place // 4][:, place % 4 * T : (place % 4 + 1) * T]

        def load_w1(e):
            nc.sync.dma_start(w1_raw[e].rearrange("p (j c) -> p j c", j=PACK), w1[e].rearrange("(p j) c -> p j c", j=PACK))

        def load_w2(e):
            nc.sync.dma_start(w2_raw[e].rearrange("p (j n) -> p j n", j=PACK), w2[e].rearrange("(p j) n -> p j n", j=PACK))

        def load_late():
            for rt in range(ROW_TILES):
                for e in range(WHOLE, E):
                    if (rt, e) == (0, WHOLE + EARLY_PARTS):
                        load_w1(E - 1)
                    rows = w2[e].rearrange("(p j) n -> p j n", j=PACK)
                    nc.sync.dma_start(part_raw(rt, e), rows[:, :, rt * P : (rt + 1) * P])
                if rt == 0:
                    for r, pos in enumerate((pos1, pos2, pos3)):
                        nc.sync.dma_start(pos_sb[r][:], pos)

        def spread_gate():
            make_identity(nc, identity[:])
            for r in range(TOP):
                bank = psum.tile([P, T], F32, name="y_bank", bufs=5)
                for c in range(T // P):
                    nc.tensor.transpose(bank[:, c * P : (c + 1) * P], gate_cols[:, r, c : c + 1].to_broadcast([P, P]), identity[:])
                nc.scalar.copy(gate_sb[:, r, :].rearrange("n (p c) -> n p c", p=P), bank[:].rearrange("n (c p) -> n p c", p=P))

        def gather_tokens(batch):
            width = GATHER_EXPERTS * C // 16
            entries = offs_sb[:, batch * width : (batch + 1) * width]
            cols = slice(batch * GATHER_EXPERTS * C, (batch + 1) * GATHER_EXPERTS * C)
            nc.vector.tensor_copy(slot_words[:, cols], tok_words[:].bitcast(U32).indirect(entries))
            nc.vector.tensor_copy(slot_scales[:, cols], tok_scales[:].bitcast(U8).indirect(entries))

        def round_w1(e):
            dst = w1_staging(e).rearrange("p (t m j) -> p m j t", t=PACK, j=PACK)
            src = w1_raw[e].rearrange("p (j m t) -> p m j t", j=PACK, t=PACK)
            copy = nc.scalar.copy if e < SCALAR_HEAD else nc.vector.tensor_copy
            copy(dst, src)

        def quantize(src, pool=stage, tag=""):
            width = src.shape[1] // PACK
            words = pool.tile([P, width], U32, name="words" + tag, align_bytes=64)
            scales = pool.tile([P, width], U8, name="scales" + tag, align_bytes=64)
            nc.vector.quantize_mx(words[:].bitcast(FP8X4), scales[:], src)
            return words, scales

        def first_product(e, words, scales):
            a_banks[e] = psum.tile([P, PACK, C], F32, name="a_bank", bufs=3)
            cols = slice(e * C, (e + 1) * C)
            for t in range(PACK):
                ch = slice(t * P, (t + 1) * P)
                nc.tensor.matmul_mx(
                    a_banks[e][:, t, :],
                    lhsT=words[:, ch].bitcast(FP8X4),
                    lhsT_scale=scales[:, ch],
                    rhs=slot_words[:, cols].bitcast(FP8X4),
                    rhs_scale=slot_scales[:, cols],
                    start=True,
                    stop=True,
                )

        def activate(e):
            dst = h_staging(e).rearrange("p (c t) -> p c t", t=PACK)
            nc.scalar.activation(dst, a_banks[e][:].rearrange("p t c -> p c t"), SILU)

        def round_w2(dst, src, copy):
            copy(dst.rearrange("p (c i j) -> p c j i", i=2, j=PACK), src.rearrange("p (j c i) -> p c j i", j=PACK, i=2))

        def multiply_w2(e, rt, words, scales):
            group = [g for g in groups if e in g][0]
            if e == 0 and rt:
                y_banks[rt, group] = y_banks[0, group, "all"][:, rt * C : (rt + 1) * C]
            elif e == 0:
                y_banks[0, group, "all"] = psum.tile([P, ROW_TILES * C], F32, name="y_bank", bufs=5)
                y_banks[rt, group] = y_banks[0, group, "all"][:, :C]
            elif e == group[0]:
                y_banks[rt, group] = psum.tile([P, len(group) * C], F32, name="y_bank", bufs=5)[:]
            place = e - group[0]
            nc.tensor.matmul_mx(
                y_banks[rt, group][:, place * C : (place + 1) * C],
                lhsT=words.bitcast(FP8X4),
                lhsT_scale=scales,
                rhs=h_mx[e][0].bitcast(FP8X4),
                rhs_scale=h_mx[e][1],
                start=True,
                stop=True,
            )

        def empty_bank(rt, group, copy=nc.scalar.copy):
            copy(y[rt][:, group[0] * C : (group[-1] + 1) * C], y_banks[rt, group])

        def second_product(e, words, scales):
            h_mx[e] = (words[:, N:], scales[:, N:])
            for rt in range(ROW_TILES):
                ch = slice(rt * P, (rt + 1) * P)
                multiply_w2(e, rt, words[:, ch], scales[:, ch])

        def round_part(rt, e, copy):
            dst = part_staging(rt, e).rearrange("p (c i j) -> p c j i", i=2, j=PACK)
            copy(dst, part_raw(rt, e).rearrange("p j (c i) -> p c j i", i=2))

        def part_products(rt, group):
            src = late_staging(rt, group)
            width = src.shape[1] // PACK
            with_h = width > len(group) * P
            tag = "kept%d" % group[0] if with_h else "late"
            words = stage.tile([P, width], U32, name="part_words", tag=tag + "_words", align_bytes=64, bufs=1 if with_h else 3)
            scales = stage.tile([P, width], U8, name="part_scales", tag=tag + "_scales", align_bytes=64, bufs=1 if with_h else 3)
            nc.vector.quantize_mx(words[:].bitcast(FP8X4), scales[:], src)
            for i, e in enumerate(group):
                first = (2 * i if with_h else i) * P
                if with_h:
                    h_mx[e] = (words[:, first + P : first + 2 * P], scales[:, first + P : first + 2 * P])
                multiply_w2(e, rt, words[:, first : first + P], scales[:, first : first + P])

        def late_row_tile(rt):
            for group in late_groups:
                for e in group:
                    round_part(rt, e, nc.scalar.copy)
                if group == late_groups[-1]:
                    for held in late_groups[:-1]:
                        empty_bank(rt, held)
                part_products(rt, group)
            empty_bank(rt, late_groups[-1])

        def entries_of(r, toks):
            return pos_sb[r][:, toks.start // 16 : toks.stop // 16]

        def fetch_gated(rt, r, toks):
            nc.vector.tensor_tensor(term(rt, r)[:, toks], y[rt][:].indirect(entries_of(r, toks)), gate_sb[:, r, toks], MULT)

        def fetch(rt, r, toks):
            nc.scalar.activation(term(rt, r)[:, toks], y[rt][:].indirect(entries_of(r, toks)), COPY)

        def apply_gate(rt, r, toks):
            nc.vector.tensor_tensor(term(rt, r)[:, toks], term(rt, r)[:, toks], gate_sb[:, r, toks], MULT)

        def add_turned(rt):
            bank = psum.tile([P, T], F32, name="a_bank", bufs=3)
            for b in range(T // P):
                toks = slice(b * P, (b + 1) * P)
                for r in range(TOP):
                    nc.tensor.matmul(bank[:, toks], term(rt, r)[:, toks], identity[:], start=r == 0, stop=r == TOP - 1, is_transpose=True)
            return [bank]

        def add_turned_apart(rt):
            sums = []
            for b in range(T // P):
                tag, bufs = ("a_bank", 3) if b % 2 else ("y_bank", 5)
                sums.append(psum.tile([P, P], F32, name="block_sum", tag=tag, bufs=bufs))
            for r in range(TOP):
                for b, bank in enumerate(sums):
                    nc.tensor.matmul(bank[:], term(rt, r)[:, b * P : (b + 1) * P], identity[:], start=r == 0, stop=r == TOP - 1, is_transpose=True)
            return sums

        def turned_sums(rt):
            return late_staging(2, late_groups[0]).bitcast(F32)[:, (1 - rt) * T : (2 - rt) * T]

        def empty_sums(rt, sums):
            width = T // len(sums)
            for b, bank in enumerate(sums):
                nc.scalar.copy(turned_sums(rt)[:, b * width : (b + 1) * width], bank[:])

        def turn_back(rt):
            turned = turned_sums(rt)
            back = psum.tile([P, T], F32, name="back", tag="y_bank", bufs=5)
            for b in range(T // P):
                nc.tensor.transpose(back[:, b * P : (b + 1) * P], turned[:, b * P : (b + 1) * P], identity[:])
            total = y[0][:, rt * T : (rt + 1) * T]
            nc.scalar.copy(total, back[:])
            queue = nc.scalar if rt else nc.sync
            queue.dma_start(out[rt * P : (rt + 1) * P, :], total)

        vector, scalar = nc.vector.tensor_copy, nc.scalar.copy
        everyone, lower, upper = slice(0, T), slice(0, HALF), slice(HALF, T)

        nc.sync.dma_start(gate_cols[:, :, : T // P], gate[:, 0, :].rearrange("r (p c) -> p r c", p=P))
        nc.vector.memset(tok_scales[:], 0)
        nc.sync.dma_start(offs_sb[:], offs)
        nc.sync.dma_start(tok_words[:], x_words[0].rearrange("p t r -> p (t r)").bitcast(I32))
        for step in range(E - 1):
            load_w1(step)
            if step == 0:
                for q in range(4):
                    nc.sync.dma_start(tok_scales[32 * q : 32 * q + 4, :], x_scales[0, 4 * q : 4 * q + 4, :].bitcast(I32))
            if 0 <= step - LAG < WHOLE:
                load_w2(step - LAG)

        spread_gate()
        for batch in range(E // GATHER_EXPERTS):
            gather_tokens(batch)
        for step in range(E):
            round_w1(step)
            if step == SCALAR_HEAD - 1:
                for e in range(step):
                    activate(e)
            if step == 7:
                load_late()
            rider = step - LAG - 1
            if step == CARRIER:
                words, scales = quantize(carried, keep, "_carried")
                first_product(step, words[:, :H], scales[:, :H])
                for e in late_groups[0]:
                    ch = slice((e - 1) * P, e * P)
                    h_mx[e] = (words[:, ch], scales[:, ch])
            elif 0 <= rider < WHOLE:
                words, scales = quantize(joint_staging(step))
                own, other = zip(halves(step, words[:]), halves(step, scales[:]))
                first_product(step, *own)
                second_product(rider, *other)
            else:
                words, scales = quantize(w1_staging(step))
                first_product(step, words[:], scales[:])
            done = step - LAG
            if 0 <= done < WHOLE:
                round_w2(second_staging(done)[:, : PACK * N], w2_raw[done], scalar)
            if step == E - 2:
                for e in range(WHOLE, WHOLE + EARLY_PARTS):
                    round_part(0, e, scalar)
            if SCALAR_HEAD - 1 <= step < E - 1:
                activate(step)
            if rider in (0, WHOLE - 1):
                for rt in range(ROW_TILES):
                    empty_bank(rt, groups[rider // 4])
        for e in (7, 8, 9):
            round_part(0, e, scalar)
        activate(E - 1)
        part_products(0, late_groups[0])
        round_part(0, 10, vector)
        round_part(0, 11, vector)
        empty_bank(0, late_groups[0])
        part_products(0, late_groups[1])
        part_products(0, late_groups[2])
        empty_bank(0, late_groups[1])
        empty_bank(0, late_groups[2], vector)
        late_row_tile(1)
        for r in range(TOP):
            fetch_gated(0, r, everyone)
        sums = add_turned(0)
        late_row_tile(2)
        empty_sums(0, sums)
        turn_back(0)
        for r in range(TOP):
            fetch_gated(1, r, everyone)
        sums = add_turned_apart(1)
        fetch(2, 2, lower)
        empty_sums(1, sums)
        fetch(2, 2, upper)
        turn_back(1)
        for toks in (lower, upper):
            fetch_gated(2, 0, toks)
            fetch_gated(2, 1, toks)
            apply_gate(2, 2, toks)
            first, second, third = [term(2, r)[:, toks] for r in range(TOP)]
            nc.vector.tensor_tensor(first, first, second, ADD)
            nc.vector.tensor_tensor(first, first, third, ADD)
            nc.sync.dma_start(out[2 * P :, toks], first)
